import numpy as np
import ml_dtypes


def mxq(x, axis, fmt="e4m3"):
    dtype, down = {"e4m3": (ml_dtypes.float8_e4m3fn, 7), "e5m2": (ml_dtypes.float8_e5m2, 14)}[fmt]
    v = np.moveaxis(np.asarray(x, np.float32).astype(ml_dtypes.bfloat16).astype(np.float64), axis, -1)
    blocks = v.reshape(v.shape[:-1] + (-1, 32))
    amax = np.abs(blocks).max(-1, keepdims=True)
    byte = np.maximum(np.where(amax > 0, np.frexp(amax)[1] - 1 + 127, 0) - down, 1)
    scale = np.exp2(byte - 127.0)
    codes = (blocks / scale).astype(np.float32).astype(dtype).astype(np.float64)
    return np.moveaxis((codes * scale).reshape(v.shape), -1, axis)


WIDE = False


def mx_kscale(k):
    if not WIDE:
        return np.ones(k)
    levels = np.array([10, -10, 5, -5, 0])
    if k % 512:
        return np.exp2(np.random.permutation(np.resize(levels, k // 32))).repeat(32)
    a = np.empty((k // 512, 16))
    for p in range(k // 512):
        a[p, :8] = np.random.permutation(np.resize(levels, 8))
        for g in range(8):
            far = levels[np.abs(levels - a[p, g]) >= 10]
            a[p, g + 8] = far[np.random.randint(len(far))]
    return np.exp2(a.ravel()).repeat(32)


def f64(x):
    return np.asarray(x).astype(np.float64)


def striped(idx):
    return np.tile(np.asarray(idx).reshape(-1, 16).T, (8, 1)).astype(np.uint16)


def unstriped(offs):
    return offs[:16].T.reshape(-1).astype(np.int64)


E2M1 = np.array([0.0, 0.5, 1.0, 1.5, 2.0, 3.0, 4.0, 6.0, -0.0, -0.5, -1.0, -1.5, -2.0, -3.0, -4.0, -6.0])


def pack_weight(w, fmt):
    k, n = w.shape
    w = f64(np.asarray(w, np.float32).astype(ml_dtypes.bfloat16)).reshape(k // 32, 32, n)
    amax = np.abs(w).max(1)
    if fmt == "e4m3":
        byte = np.frexp(amax)[1] - 1 + 127 - 7
    else:
        mant, ex = np.frexp(amax / 6.0)
        byte = np.where(mant > 0.5, ex, ex - 1) + 127
    byte = np.clip(np.where(amax > 0, byte, 1), 1, 254)
    scaled = (w * np.exp2(127.0 - byte)[:, None, :]).reshape(k, n).astype(np.float32)
    by_word = np.ascontiguousarray(scaled.reshape(k // 512, 128, 4, n).transpose(0, 1, 3, 2))
    if fmt == "e4m3":
        words = by_word.astype(ml_dtypes.float8_e4m3fn).view(np.uint8)
    else:
        c = by_word.astype(ml_dtypes.float4_e2m1fn).view(np.uint8) & 0xF
        words = (c[..., 0::2] | (c[..., 1::2] << 4)).reshape(k // 512, 128, 2 * n)
    return np.ascontiguousarray(words), np.ascontiguousarray(byte.astype(np.uint8).reshape(k // 512, 16, n))


def unpack_weight(words, scales, fmt):
    g, _, n = scales.shape
    words = np.ascontiguousarray(words).reshape(g, 128, n, -1)
    if fmt == "e4m3":
        vals = words.view(ml_dtypes.float8_e4m3fn).astype(np.float64)
    else:
        nib = np.empty((g, 128, n, 4), np.uint8)
        nib[..., 0::2] = words & 0xF
        nib[..., 1::2] = words >> 4
        vals = E2M1[nib]
    vals = vals * np.repeat(np.exp2(scales.astype(np.float64) - 127.0), 8, axis=1)[..., None]
    return vals.transpose(0, 1, 3, 2).reshape(g * 512, n)


def silu(v):
    return v / (1.0 + np.exp(-v))


def bf(x):
    return np.asarray(x, np.float32).astype(ml_dtypes.bfloat16)


def planes(Y):
    r, m = Y.shape
    b = f64(bf(Y)).reshape(r // 32, 32, m)
    amax = np.abs(b).max(1)
    byte = np.clip(np.where(amax > 0, np.frexp(amax)[1] - 1 + 127 - 7, 1), 1, 254)
    codes = (b * np.exp2(127.0 - byte)[:, None, :]).reshape(r, m).astype(np.float32).astype(ml_dtypes.float8_e4m3fn).view(np.uint8)
    words = codes.reshape(r // 512, 128, 4, m).transpose(0, 1, 3, 2)
    return np.ascontiguousarray(words), np.ascontiguousarray(byte.astype(np.uint8).reshape(r // 512, 16, m))


B, N, T, D, NQ = 1, 512, 2048, 512, 512


def setup_inputs():
    n = np.random.standard_normal
    idx = np.random.permutation(T)[:B * N]
    s = mx_kscale(D)[:, None]
    kp = pack_weight(n((D, T)) / s, "e4m3")
    cp = pack_weight(n((D, T)) / s, "e4m3")
    return {
        "qT": (n((B, D, NQ)) * s * (1.00 / np.sqrt(D))).astype(np.float32),
        "k_words": kp[0],
        "k_scales": kp[1],
        "c_words": cp[0],
        "c_scales": cp[1],
        "offs": striped(idx),
    }


def reference(qT, k_words, k_scales, c_words, c_scales, offs):
    idx = unstriped(offs)
    pick = lambda x, which: x[:, which].reshape(x.shape[0], B, -1).transpose(1, 0, 2)
    k = unpack_weight(k_words, k_scales, "e4m3")
    kg = pick(k, idx)
    c = unpack_weight(c_words, c_scales, "e4m3")
    cg = pick(c, idx)
    qq = mxq(f64(qT), 1, "e4m3")
    a = kg.transpose(0, 2, 1) @ qq
    z = cg.transpose(0, 2, 1) @ qq
    y = silu(a) * z
    Y = y[0]
    words, scales = planes(Y)
    return Y, words, scales

@@ -1,0 +1,139 @@
+from contextlib import ExitStack
+
+import concourse.mybir as mybir
+
+F32 = mybir.dt.float32
+BF16 = mybir.dt.bfloat16
+I32 = mybir.dt.int32
+U32 = mybir.dt.uint32
+U16 = mybir.dt.uint16
+U8 = mybir.dt.uint8
+FP8X4 = mybir.dt.float8_e4m3fn_x4
+ACT = mybir.ActivationFunctionType
+MULT = mybir.AluOpType.mult
+
+P = 128
+PACK = 4
+SLOTS = 512
+NEURONS = 2048
+QUERIES = 512
+CHUNK = 128
+HALF = 256
+
+FLOPS = 2 * 2 * 512 * 512 * 512
+
+
+def tile_attend_plh_swiglu_topk_kernel(tc, qT, k_words, k_scales, c_words, c_scales, offs, out_0, out_1, out_2):
+    nc = tc.nc
+    with ExitStack() as ctx:
+        keep = ctx.enter_context(tc.tile_pool(name="keep", bufs=1))
+        psum = ctx.enter_context(tc.psum_pool(name="psum", bufs=1))
+
+        offsets = keep.tile([P, SLOTS // 16], U16, name="offsets")
+        kw = keep.tile([P, NEURONS], I32, name="kw")
+        cw = keep.tile([P, NEURONS], I32, name="cw")
+        ks = keep.tile([P, NEURONS], U8, name="ks")
+        cs = keep.tile([P, NEURONS], U8, name="cs", tag="cs_then_q", align_bytes=64)
+        q_raw = [keep.tile([P, PACK, HALF], F32, name=f"q_raw{h}") for h in range(2)]
+        q_rows = qT[0].rearrange("(p t) q -> p t q", t=PACK)
+
+        nc.gpsimd.memset(ks[:].bitcast(I32), 0)
+        nc.vector.memset(cs[:].bitcast(I32), 0)
+
+        nc.sync.dma_start(offsets[:], offs)
+        nc.sync.dma_start(kw[:], k_words[0].rearrange("p n t -> p (n t)").bitcast(I32))
+        for quad in range(4):
+            nc.scalar.dma_start(ks[32 * quad : 32 * quad + 4, :].bitcast(I32), k_scales[0, 4 * quad : 4 * quad + 4, :].bitcast(I32))
+        for quad in range(4):
+            nc.gpsimd.dma_start(cs[32 * quad + 4 : 32 * quad + 8, :].bitcast(I32), c_scales[0, 4 * quad : 4 * quad + 4, :].bitcast(I32))
+        nc.sync.dma_start(q_raw[0][:], q_rows[:, :, 0:HALF])
+        nc.sync.dma_start(q_raw[1][:], q_rows[:, :, HALF:QUERIES])
+        nc.sync.dma_start(cw[:], c_words[0].rearrange("p n t -> p (n t)").bitcast(I32))
+
+        warm = keep.tile([P, 2], F32, name="warm")
+        nc.vector.memset(warm[:, 0:1], 0.0)
+        nc.scalar.activation(warm[:, 1:2], warm[:, 0:1], ACT.Silu)
+
+        def gather_scales(table, name):
+            listed = keep.tile([P, SLOTS], U8, name=name + "_listed", tag=name[0] + "_gathered", align_bytes=64)
+            dealt = keep.tile([P, SLOTS], U8, name=name + "_dealt", align_bytes=64)
+            nc.vector.tensor_copy(listed[:], table[:].indirect(offsets[:]))
+            nc.vector.tensor_copy(dealt[:].rearrange("p (r s) -> p r s", r=PACK), listed[:].rearrange("p (s r) -> p r s", r=PACK))
+            return dealt
+
+        def gather_words(table, name):
+            dealt = keep.tile([P, SLOTS], U32, name=name + "_dealt", tag=name[0] + "_gathered", align_bytes=64)
+            nc.vector.tensor_copy(dealt[:].rearrange("p (r s) -> p s r", r=PACK), table[:].bitcast(U32).indirect(offsets[:]))
+            return dealt
+
+        q_bf = [keep.tile([P, HALF, PACK], BF16, name=f"q_bf{h}", align_bytes=64) for h in range(2)]
+        q_codes = []
+        q_scale = [keep.tile([P, HALF], U8, name=f"q_scale{h}", align_bytes=64) for h in range(2)]
+
+        def round_q(h):
+            nc.scalar.copy(q_bf[h][:].rearrange("p (c i) t -> p c t i", i=4), q_raw[h][:].rearrange("p t (c i) -> p c t i", i=4))
+
+        def quantise_q(h):
+            q_codes.append(keep.tile([P, HALF], U32, name=f"q_codes{h}", tag="cs_then_q" if h == 1 else "q_codes", align_bytes=64))
+            nc.vector.quantize_mx(q_codes[h][:].bitcast(FP8X4), q_scale[h][:], q_bf[h][:].rearrange("p q t -> p (q t)"))
+
+        def product(name, words, scales, row0, c):
+            bank = psum.tile([P, PACK, CHUNK], F32, name=f"{name}{c}")
+            h, cols = divmod(c * CHUNK, HALF)
+            for r in range(PACK):
+                nc.tensor.matmul_mx(
+                    bank[:, r, :],
+                    lhsT=words[:, r * P : (r + 1) * P].bitcast(FP8X4),
+                    lhsT_scale=scales[row0:P, r * P : (r + 1) * P],
+                    rhs=q_codes[h][:, cols : cols + CHUNK].bitcast(FP8X4),
+                    rhs_scale=q_scale[h][:, cols : cols + CHUNK],
+                    start=True,
+                    stop=True,
+                )
+            return bank
+
+        out_rows = out_0.rearrange("(p r) q -> p r q", r=PACK)
+        y_codes = keep.tile([P, QUERIES], U32, name="y_codes", align_bytes=64)
+        y_scale = keep.tile([P, QUERIES], U8, name="y_scale", align_bytes=64)
+        words_out = out_1[0].rearrange("p q u -> p (q u)").bitcast(I32)
+
+        def gate(c, bank):
+            g = keep.tile([P, PACK, CHUNK], F32, name=f"gate{c}")
+            nc.scalar.activation(g[:], bank[:], ACT.Silu)
+            return g
+
+        def multiply(c, g, bank):
+            y = keep.tile([P, PACK, CHUNK], F32, name=f"y{c}")
+            nc.vector.tensor_tensor(y[:], bank[:], g[:], MULT)
+            nc.sync.dma_start(out_rows[:, :, c * CHUNK : (c + 1) * CHUNK], y[:])
+            return y
+
+        y_bf = keep.tile([P, QUERIES * PACK], BF16, name="y_bf", align_bytes=64)
+
+        def round_y(c, y):
+            dst = y_bf[:, c * CHUNK * PACK : (c + 1) * CHUNK * PACK].rearrange("p (c i t) -> p c t i", i=4, t=PACK)
+            nc.scalar.copy(dst, y[:].rearrange("p t (c i) -> p c t i", i=4))
+
+        def quantise_y(lo, hi):
+            nc.vector.quantize_mx(y_codes[:, lo:hi].bitcast(FP8X4), y_scale[:, lo:hi], y_bf[:, lo * PACK : hi * PACK])
+
+        ksd = gather_scales(ks, "ks")
+        kwd = gather_words(kw, "kw")
+        round_q(0)
+        round_q(1)
+        quantise_q(0)
+        csd = gather_scales(cs, "cs")
+        quantise_q(1)
+        cwd = gather_words(cw, "cw")
+        gates = [gate(c, product("a", kwd, ksd, 0, c)) for c in range(4)]
+        ys = [multiply(c, gates[c], product("z", cwd, csd, 4, c)) for c in range(4)]
+        for c in range(4):
+            round_y(c, ys[c])
+        quantise_y(0, 2 * CHUNK)
+        nc.sync.dma_start(words_out[:, 0:HALF], y_codes[:, 0:HALF].bitcast(I32))
+        quantise_y(2 * CHUNK, 3 * CHUNK)
+        quantise_y(3 * CHUNK, 4 * CHUNK)
+        nc.sync.dma_start(words_out[:, HALF:QUERIES], y_codes[:, HALF:QUERIES].bitcast(I32))
+        for quad in range(4):
+            queue = nc.scalar if quad % 2 == 0 else nc.sync
+            queue.dma_start(out_2[0, 4 * quad : 4 * quad + 4, :].bitcast(I32), y_scale[32 * quad : 32 * quad + 4, :].bitcast(I32))

@@ -32,22 +32,25 @@ def tile_attend_plh_swiglu_topk_kernel(tc, qT, k_words, k_scales, c_words, c_sca
         offsets = keep.tile([P, SLOTS // 16], U16, name="offsets")
         kw = keep.tile([P, NEURONS], I32, name="kw")
         cw = keep.tile([P, NEURONS], I32, name="cw")
-        ks = keep.tile([P, NEURONS], U8, name="ks")
-        cs = keep.tile([P, NEURONS], U8, name="cs", tag="cs_then_q", align_bytes=64)
-        q_raw = [keep.tile([P, PACK, HALF], F32, name=f"q_raw{h}") for h in range(2)]
+        ks = keep.tile([P, NEURONS], U8, name="ks", tag="scales_then_q0", align_bytes=64)
+        cs = keep.tile([P, NEURONS], U8, name="cs", tag="scales_then_q1", align_bytes=64)
+        q_raw = [keep.tile([P, PACK, HALF], F32, name=f"q_raw{h}", tag=f"q_then_gate{h}") for h in range(2)]
         q_rows = qT[0].rearrange("(p t) q -> p t q", t=PACK)
 
-        nc.gpsimd.memset(ks[:].bitcast(I32), 0)
+        nc.vector.memset(ks[:].bitcast(I32), 0)
         nc.vector.memset(cs[:].bitcast(I32), 0)
 
+        def load_scales(table, rows, row0):
+            for quad in range(4):
+                first = 32 * quad + row0
+                nc.sync.dma_start(table[first : first + 4, :].bitcast(I32), rows[0, 4 * quad : 4 * quad + 4, :].bitcast(I32))
+
         nc.sync.dma_start(offsets[:], offs)
-        nc.sync.dma_start(kw[:], k_words[0].rearrange("p n t -> p (n t)").bitcast(I32))
-        for quad in range(4):
-            nc.scalar.dma_start(ks[32 * quad : 32 * quad + 4, :].bitcast(I32), k_scales[0, 4 * quad : 4 * quad + 4, :].bitcast(I32))
-        for quad in range(4):
-            nc.gpsimd.dma_start(cs[32 * quad + 4 : 32 * quad + 8, :].bitcast(I32), c_scales[0, 4 * quad : 4 * quad + 4, :].bitcast(I32))
         nc.sync.dma_start(q_raw[0][:], q_rows[:, :, 0:HALF])
+        load_scales(ks, k_scales, 0)
+        nc.sync.dma_start(kw[:], k_words[0].rearrange("p n t -> p (n t)").bitcast(I32))
         nc.sync.dma_start(q_raw[1][:], q_rows[:, :, HALF:QUERIES])
+        load_scales(cs, c_scales, 4)
         nc.sync.dma_start(cw[:], c_words[0].rearrange("p n t -> p (n t)").bitcast(I32))
 
         warm = keep.tile([P, 2], F32, name="warm")
@@ -74,7 +77,7 @@ def tile_attend_plh_swiglu_topk_kernel(tc, qT, k_words, k_scales, c_words, c_sca
             nc.scalar.copy(q_bf[h][:].rearrange("p (c i) t -> p c t i", i=4), q_raw[h][:].rearrange("p t (c i) -> p c t i", i=4))
 
         def quantise_q(h):
-            q_codes.append(keep.tile([P, HALF], U32, name=f"q_codes{h}", tag="cs_then_q" if h == 1 else "q_codes", align_bytes=64))
+            q_codes.append(keep.tile([P, HALF], U32, name=f"q_codes{h}", tag=f"scales_then_q{h}", align_bytes=64))
             nc.vector.quantize_mx(q_codes[h][:].bitcast(FP8X4), q_scale[h][:], q_bf[h][:].rearrange("p q t -> p (q t)"))
 
         def product(name, words, scales, row0, c):
@@ -98,7 +101,7 @@ def tile_attend_plh_swiglu_topk_kernel(tc, qT, k_words, k_scales, c_words, c_sca
         words_out = out_1[0].rearrange("p q u -> p (q u)").bitcast(I32)
 
         def gate(c, bank):
-            g = keep.tile([P, PACK, CHUNK], F32, name=f"gate{c}")
+            g = keep.tile([P, PACK, CHUNK], F32, name=f"gate{c}", tag=f"q_then_gate{1 - c}")
             nc.scalar.activation(g[:], bank[:], ACT.Silu)
             return g
 
@@ -118,10 +121,10 @@ def tile_attend_plh_swiglu_topk_kernel(tc, qT, k_words, k_scales, c_words, c_sca
             nc.vector.quantize_mx(y_codes[:, lo:hi].bitcast(FP8X4), y_scale[:, lo:hi], y_bf[:, lo * PACK : hi * PACK])
 
         ksd = gather_scales(ks, "ks")
-        kwd = gather_words(kw, "kw")
         round_q(0)
-        round_q(1)
         quantise_q(0)
+        kwd = gather_words(kw, "kw")
+        round_q(1)
         csd = gather_scales(cs, "cs")
         quantise_q(1)
         cwd = gather_words(cw, "cw")

@@ -31,112 +31,122 @@ def tile_attend_plh_swiglu_topk_kernel(tc, qT, k_words, k_scales, c_words, c_sca
 
         offsets = keep.tile([P, SLOTS // 16], U16, name="offsets")
         kw = keep.tile([P, NEURONS], I32, name="kw")
-        cw = keep.tile([P, NEURONS], I32, name="cw")
+        cw = keep.tile([P, NEURONS], I32, name="cw", tag="words_then_q", align_bytes=64)
         ks = keep.tile([P, NEURONS], U8, name="ks", tag="scales_then_q0", align_bytes=64)
         cs = keep.tile([P, NEURONS], U8, name="cs", tag="scales_then_q1", align_bytes=64)
-        q_raw = [keep.tile([P, PACK, HALF], F32, name=f"q_raw{h}", tag=f"q_then_gate{h}") for h in range(2)]
+        q_first = keep.tile([P, PACK, HALF], F32, name="q_first")
+        q_mid = keep.tile([P, PACK, CHUNK], F32, name="q_mid", tag="q_then_gate1", align_bytes=64)
+        q_late = keep.tile([P, PACK, CHUNK], F32, name="q_late", tag="q_then_gate0", align_bytes=64)
         q_rows = qT[0].rearrange("(p t) q -> p t q", t=PACK)
 
         nc.vector.memset(ks[:].bitcast(I32), 0)
         nc.vector.memset(cs[:].bitcast(I32), 0)
 
         def load_scales(table, rows, row0):
-            for quad in range(4):
-                first = 32 * quad + row0
-                nc.sync.dma_start(table[first : first + 4, :].bitcast(I32), rows[0, 4 * quad : 4 * quad + 4, :].bitcast(I32))
+            for i in range(4):
+                nc.sync.dma_start(table[row0 + i : P : 32, :].bitcast(I32), rows[0, i:16:4, :].bitcast(I32))
 
         nc.sync.dma_start(offsets[:], offs)
-        nc.sync.dma_start(q_raw[0][:], q_rows[:, :, 0:HALF])
+        nc.sync.dma_start(q_first[:], q_rows[:, :, CHUNK : CHUNK + HALF])
         load_scales(ks, k_scales, 0)
         nc.sync.dma_start(kw[:], k_words[0].rearrange("p n t -> p (n t)").bitcast(I32))
-        nc.sync.dma_start(q_raw[1][:], q_rows[:, :, HALF:QUERIES])
+        nc.sync.dma_start(q_mid[:], q_rows[:, :, 0:CHUNK])
         load_scales(cs, c_scales, 4)
         nc.sync.dma_start(cw[:], c_words[0].rearrange("p n t -> p (n t)").bitcast(I32))
+        nc.sync.dma_start(q_late[:], q_rows[:, :, HALF + CHUNK : QUERIES])
 
         warm = keep.tile([P, 2], F32, name="warm")
         nc.vector.memset(warm[:, 0:1], 0.0)
         nc.scalar.activation(warm[:, 1:2], warm[:, 0:1], ACT.Silu)
 
-        def gather_scales(table, name):
-            listed = keep.tile([P, SLOTS], U8, name=name + "_listed", tag=name[0] + "_gathered", align_bytes=64)
+        def gather_scales(table, name, between):
+            listed = keep.tile([P, SLOTS], U8, name=name + "_listed")
             dealt = keep.tile([P, SLOTS], U8, name=name + "_dealt", align_bytes=64)
             nc.vector.tensor_copy(listed[:], table[:].indirect(offsets[:]))
+            between()
             nc.vector.tensor_copy(dealt[:].rearrange("p (r s) -> p r s", r=PACK), listed[:].rearrange("p (s r) -> p r s", r=PACK))
             return dealt
 
         def gather_words(table, name):
-            dealt = keep.tile([P, SLOTS], U32, name=name + "_dealt", tag=name[0] + "_gathered", align_bytes=64)
+            dealt = keep.tile([P, SLOTS], U32, name=name + "_dealt", align_bytes=64)
             nc.vector.tensor_copy(dealt[:].rearrange("p (r s) -> p s r", r=PACK), table[:].bitcast(U32).indirect(offsets[:]))
             return dealt
 
-        q_bf = [keep.tile([P, HALF, PACK], BF16, name=f"q_bf{h}", align_bytes=64) for h in range(2)]
-        q_codes = []
-        q_scale = [keep.tile([P, HALF], U8, name=f"q_scale{h}", align_bytes=64) for h in range(2)]
+        q_parts = {}
 
-        def round_q(h):
-            nc.scalar.copy(q_bf[h][:].rearrange("p (c i) t -> p c t i", i=4), q_raw[h][:].rearrange("p t (c i) -> p c t i", i=4))
+        def round_q(raw, lo, width):
+            q_bf = keep.tile([P, width, PACK], BF16, name=f"q_bf{len(q_parts)}", tag=f"q_bf{width}", align_bytes=64)
+            nc.scalar.copy(q_bf[:].rearrange("p (c i) t -> p c t i", i=4), raw[:, :, lo : lo + width].rearrange("p t (c i) -> p c t i", i=4))
+            return q_bf
 
-        def quantise_q(h):
-            q_codes.append(keep.tile([P, HALF], U32, name=f"q_codes{h}", tag=f"scales_then_q{h}", align_bytes=64))
-            nc.vector.quantize_mx(q_codes[h][:].bitcast(FP8X4), q_scale[h][:], q_bf[h][:].rearrange("p q t -> p (q t)"))
+        def quantise_q(q_bf, width, slot, chunk):
+            codes = keep.tile([P, width], U32, name=f"q_codes{len(q_parts)}", tag=slot, align_bytes=64)
+            scale = keep.tile([P, width], U8, name=f"q_scale{len(q_parts)}", align_bytes=64)
+            nc.vector.quantize_mx(codes[:].bitcast(FP8X4), scale[:], q_bf[:].rearrange("p q t -> p (q t)"))
+            for lo in range(0, width, CHUNK):
+                q_parts[chunk + lo // CHUNK] = (codes[:, lo : lo + CHUNK], scale[:, lo : lo + CHUNK])
 
         def product(name, words, scales, row0, c):
-            bank = psum.tile([P, PACK, CHUNK], F32, name=f"{name}{c}")
-            h, cols = divmod(c * CHUNK, HALF)
+            bank = psum.tile([P, PACK, CHUNK], F32, name=f"{name}{c}", tag="a0" if (name, c) == ("z", 2) else f"{name}{c}")
+            codes, scale = q_parts[c]
             for r in range(PACK):
                 nc.tensor.matmul_mx(
                     bank[:, r, :],
                     lhsT=words[:, r * P : (r + 1) * P].bitcast(FP8X4),
                     lhsT_scale=scales[row0:P, r * P : (r + 1) * P],
-                    rhs=q_codes[h][:, cols : cols + CHUNK].bitcast(FP8X4),
-                    rhs_scale=q_scale[h][:, cols : cols + CHUNK],
+                    rhs=codes.bitcast(FP8X4),
+                    rhs_scale=scale,
                     start=True,
                     stop=True,
                 )
             return bank
 
         out_rows = out_0.rearrange("(p r) q -> p r q", r=PACK)
-        y_codes = keep.tile([P, QUERIES], U32, name="y_codes", align_bytes=64)
         y_scale = keep.tile([P, QUERIES], U8, name="y_scale", align_bytes=64)
         words_out = out_1[0].rearrange("p q u -> p (q u)").bitcast(I32)
 
         def gate(c, bank):
-            g = keep.tile([P, PACK, CHUNK], F32, name=f"gate{c}", tag=f"q_then_gate{1 - c}")
+            g = keep.tile([P, PACK, CHUNK], F32, name=f"gate{c}", tag=f"q_then_gate{c}", align_bytes=64)
             nc.scalar.activation(g[:], bank[:], ACT.Silu)
             return g
 
         def multiply(c, g, bank):
-            y = keep.tile([P, PACK, CHUNK], F32, name=f"y{c}")
+            y = keep.tile([P, PACK, CHUNK], F32, name=f"y{c}", tag={1: f"q_bf{CHUNK}", 2: "q_then_gate1"}.get(c, f"y{c}"), align_bytes=64)
             nc.vector.tensor_tensor(y[:], bank[:], g[:], MULT)
             nc.sync.dma_start(out_rows[:, :, c * CHUNK : (c + 1) * CHUNK], y[:])
             return y
 
         y_bf = keep.tile([P, QUERIES * PACK], BF16, name="y_bf", align_bytes=64)
 
-        def round_y(c, y):
+        def round_y(c, y, copy):
             dst = y_bf[:, c * CHUNK * PACK : (c + 1) * CHUNK * PACK].rearrange("p (c i t) -> p c t i", i=4, t=PACK)
-            nc.scalar.copy(dst, y[:].rearrange("p t (c i) -> p c t i", i=4))
+            copy(dst, y[:].rearrange("p t (c i) -> p c t i", i=4))
 
-        def quantise_y(lo, hi):
+        def quantise_y(y_codes, lo, hi):
             nc.vector.quantize_mx(y_codes[:, lo:hi].bitcast(FP8X4), y_scale[:, lo:hi], y_bf[:, lo * PACK : hi * PACK])
 
-        ksd = gather_scales(ks, "ks")
-        round_q(0)
-        quantise_q(0)
+        ksd = gather_scales(ks, "ks", lambda: quantise_q(round_q(q_first, 0, HALF), HALF, "scales_then_q0", 1))
         kwd = gather_words(kw, "kw")
-        round_q(1)
-        csd = gather_scales(cs, "cs")
-        quantise_q(1)
+        csd = gather_scales(cs, "cs", lambda: quantise_q(round_q(q_mid, 0, CHUNK), CHUNK, "scales_then_q1", 0))
         cwd = gather_words(cw, "cw")
-        gates = [gate(c, product("a", kwd, ksd, 0, c)) for c in range(4)]
-        ys = [multiply(c, gates[c], product("z", cwd, csd, 4, c)) for c in range(4)]
-        for c in range(4):
-            round_y(c, ys[c])
-        quantise_y(0, 2 * CHUNK)
-        nc.sync.dma_start(words_out[:, 0:HALF], y_codes[:, 0:HALF].bitcast(I32))
-        quantise_y(2 * CHUNK, 3 * CHUNK)
-        quantise_y(3 * CHUNK, 4 * CHUNK)
-        nc.sync.dma_start(words_out[:, HALF:QUERIES], y_codes[:, HALF:QUERIES].bitcast(I32))
+        gates = {c: gate(c, product("a", kwd, ksd, 0, c)) for c in (1, 2)}
+        late = round_q(q_late, 0, CHUNK)
+        gates[0] = gate(0, product("a", kwd, ksd, 0, 0))
+        quantise_q(late, CHUNK, "words_then_q", 3)
+        z = {1: product("z", cwd, csd, 4, 1)}
+        gates[3] = gate(3, product("a", kwd, ksd, 0, 3))
+        for c in (0, 2, 3):
+            z[c] = product("z", cwd, csd, 4, c)
+        ys = {c: multiply(c, gates[c], z[c]) for c in (1, 0, 2, 3)}
+        for c in (1, 0, 2):
+            round_y(c, ys[c], nc.scalar.copy)
+        y_codes = keep.tile([P, QUERIES], U32, name="y_codes", tag="q_then_gate2", align_bytes=64)
+        quantise_y(y_codes, 0, 2 * CHUNK)
+        round_y(3, ys[3], nc.vector.tensor_copy)
+        quantise_y(y_codes, 2 * CHUNK, 3 * CHUNK)
+        nc.sync.dma_start(words_out[:, 0 : 3 * CHUNK], y_codes[:, 0 : 3 * CHUNK].bitcast(I32))
+        quantise_y(y_codes, 3 * CHUNK, 4 * CHUNK)
+        nc.sync.dma_start(words_out[:, 3 * CHUNK : QUERIES], y_codes[:, 3 * CHUNK : QUERIES].bitcast(I32))
         for quad in range(4):
             queue = nc.scalar if quad % 2 == 0 else nc.sync
             queue.dma_start(out_2[0, 4 * quad : 4 * quad + 4, :].bitcast(I32), y_scale[32 * quad : 32 * quad + 4, :].bitcast(I32))

@@ -55,10 +55,6 @@ def tile_attend_plh_swiglu_topk_kernel(tc, qT, k_words, k_scales, c_words, c_sca
         nc.sync.dma_start(cw[:], c_words[0].rearrange("p n t -> p (n t)").bitcast(I32))
         nc.sync.dma_start(q_late[:], q_rows[:, :, HALF + CHUNK : QUERIES])
 
-        warm = keep.tile([P, 2], F32, name="warm")
-        nc.vector.memset(warm[:, 0:1], 0.0)
-        nc.scalar.activation(warm[:, 1:2], warm[:, 0:1], ACT.Silu)
-
         def gather_scales(table, name, between):
             listed = keep.tile([P, SLOTS], U8, name=name + "_listed")
             dealt = keep.tile([P, SLOTS], U8, name=name + "_dealt", align_bytes=64)

@@ -19,6 +19,8 @@ NEURONS = 2048
 QUERIES = 512
 CHUNK = 128
 HALF = 256
+BLOCKS = 16
+ROW0 = P - BLOCKS
 
 FLOPS = 2 * 2 * 512 * 512 * 512
 
@@ -31,118 +33,121 @@ def tile_attend_plh_swiglu_topk_kernel(tc, qT, k_words, k_scales, c_words, c_sca
 
         offsets = keep.tile([P, SLOTS // 16], U16, name="offsets")
         kw = keep.tile([P, NEURONS], I32, name="kw")
-        cw = keep.tile([P, NEURONS], I32, name="cw", tag="words_then_q", align_bytes=64)
-        ks = keep.tile([P, NEURONS], U8, name="ks", tag="scales_then_q0", align_bytes=64)
-        cs = keep.tile([P, NEURONS], U8, name="cs", tag="scales_then_q1", align_bytes=64)
+        cw = keep.tile([P, NEURONS], I32, name="cw")
+        ks = keep.tile([P, NEURONS], U8, name="ks")
+        cs = keep.tile([P, NEURONS], U8, name="cs")
         q_first = keep.tile([P, PACK, HALF], F32, name="q_first")
-        q_mid = keep.tile([P, PACK, CHUNK], F32, name="q_mid", tag="q_then_gate1", align_bytes=64)
-        q_late = keep.tile([P, PACK, CHUNK], F32, name="q_late", tag="q_then_gate0", align_bytes=64)
         q_rows = qT[0].rearrange("(p t) q -> p t q", t=PACK)
 
         nc.vector.memset(ks[:].bitcast(I32), 0)
-        nc.vector.memset(cs[:].bitcast(I32), 0)
-
-        def load_scales(table, rows, row0):
-            for i in range(4):
-                nc.sync.dma_start(table[row0 + i : P : 32, :].bitcast(I32), rows[0, i:16:4, :].bitcast(I32))
-
+        nc.vector.memset(cs[0:ROW0, :].bitcast(I32), 0)
         nc.sync.dma_start(offsets[:], offs)
-        nc.sync.dma_start(q_first[:], q_rows[:, :, CHUNK : CHUNK + HALF])
-        load_scales(ks, k_scales, 0)
+        nc.sync.dma_start(cs[ROW0:P, :].bitcast(I32), c_scales[0].bitcast(I32))
+        nc.sync.dma_start(q_first[:], q_rows[:, :, 0:HALF])
+        for i in range(4):
+            nc.sync.dma_start(ks[i:P:32, :].bitcast(I32), k_scales[0, i:16:4, :].bitcast(I32))
         nc.sync.dma_start(kw[:], k_words[0].rearrange("p n t -> p (n t)").bitcast(I32))
-        nc.sync.dma_start(q_mid[:], q_rows[:, :, 0:CHUNK])
-        load_scales(cs, c_scales, 4)
         nc.sync.dma_start(cw[:], c_words[0].rearrange("p n t -> p (n t)").bitcast(I32))
-        nc.sync.dma_start(q_late[:], q_rows[:, :, HALF + CHUNK : QUERIES])
 
-        def gather_scales(table, name, between):
-            listed = keep.tile([P, SLOTS], U8, name=name + "_listed")
-            dealt = keep.tile([P, SLOTS], U8, name=name + "_dealt", align_bytes=64)
-            nc.vector.tensor_copy(listed[:], table[:].indirect(offsets[:]))
-            between()
-            nc.vector.tensor_copy(dealt[:].rearrange("p (r s) -> p r s", r=PACK), listed[:].rearrange("p (s r) -> p r s", r=PACK))
-            return dealt
+        k_listed = keep.tile([P, SLOTS], U8, name="k_listed")
+        c_listed = keep.tile([P, SLOTS], U8, name="c_listed", tag="listed_then_q")
+        k_plane = keep.tile([P, SLOTS], U8, name="k_plane", align_bytes=64)
+        c_plane = keep.tile([P, SLOTS], U8, name="c_plane", align_bytes=64)
+        nc.vector.tensor_copy(c_listed[:], cs[:].indirect(offsets[:]))
+        nc.vector.tensor_copy(c_plane[:].rearrange("p (r s) -> p r s", r=PACK), c_listed[:].rearrange("p (s r) -> p r s", r=PACK))
+        for quad in range(4):
+            nc.sync.dma_start(c_plane[32 * quad : 32 * quad + 4, :].bitcast(I32), c_plane[ROW0 + 4 * quad : ROW0 + 4 * quad + 4, :].bitcast(I32))
+        q_late = keep.tile([P, PACK, HALF], F32, name="q_late", tag="listed_then_q")
+        q_third, q_last = q_late[:, :, 0:CHUNK], q_late[:, :, CHUNK:HALF]
+        nc.sync.dma_start(q_late[:], q_rows[:, :, HALF:QUERIES])
+        nc.vector.tensor_copy(k_listed[:], ks[:].indirect(offsets[:]))
 
         def gather_words(table, name):
             dealt = keep.tile([P, SLOTS], U32, name=name + "_dealt", align_bytes=64)
             nc.vector.tensor_copy(dealt[:].rearrange("p (r s) -> p s r", r=PACK), table[:].bitcast(U32).indirect(offsets[:]))
             return dealt
 
-        q_parts = {}
+        q_codes = keep.tile([P, QUERIES], U32, name="q_codes", align_bytes=64)
+        q_scale = keep.tile([P, QUERIES], U8, name="q_scale", align_bytes=64)
 
-        def round_q(raw, lo, width):
-            q_bf = keep.tile([P, width, PACK], BF16, name=f"q_bf{len(q_parts)}", tag=f"q_bf{width}", align_bytes=64)
-            nc.scalar.copy(q_bf[:].rearrange("p (c i) t -> p c t i", i=4), raw[:, :, lo : lo + width].rearrange("p t (c i) -> p c t i", i=4))
+        def round_q(raw, q_bf, copy):
+            copy(q_bf.rearrange("p (c i t) -> p c t i", i=4, t=PACK), raw.rearrange("p t (c i) -> p c t i", i=4))
             return q_bf
 
-        def quantise_q(q_bf, width, slot, chunk):
-            codes = keep.tile([P, width], U32, name=f"q_codes{len(q_parts)}", tag=slot, align_bytes=64)
-            scale = keep.tile([P, width], U8, name=f"q_scale{len(q_parts)}", align_bytes=64)
-            nc.vector.quantize_mx(codes[:].bitcast(FP8X4), scale[:], q_bf[:].rearrange("p q t -> p (q t)"))
-            for lo in range(0, width, CHUNK):
-                q_parts[chunk + lo // CHUNK] = (codes[:, lo : lo + CHUNK], scale[:, lo : lo + CHUNK])
+        def quantise_q(q_bf, lo, hi):
+            nc.vector.quantize_mx(q_codes[:, lo:hi].bitcast(FP8X4), q_scale[:, lo:hi], q_bf)
 
-        def product(name, words, scales, row0, c):
-            bank = psum.tile([P, PACK, CHUNK], F32, name=f"{name}{c}", tag="a0" if (name, c) == ("z", 2) else f"{name}{c}")
-            codes, scale = q_parts[c]
-            for r in range(PACK):
+        def product(name, words, plane, rows, lo, hi):
+            bank = psum.tile([P, len(rows), hi - lo], F32, name=name)
+            for j, r in enumerate(rows):
                 nc.tensor.matmul_mx(
-                    bank[:, r, :],
+                    bank[:, j, :],
                     lhsT=words[:, r * P : (r + 1) * P].bitcast(FP8X4),
-                    lhsT_scale=scales[row0:P, r * P : (r + 1) * P],
-                    rhs=codes.bitcast(FP8X4),
-                    rhs_scale=scale,
+                    lhsT_scale=plane[:, r * P : (r + 1) * P],
+                    rhs=q_codes[:, lo:hi].bitcast(FP8X4),
+                    rhs_scale=q_scale[:, lo:hi],
                     start=True,
                     stop=True,
                 )
             return bank
 
         out_rows = out_0.rearrange("(p r) q -> p r q", r=PACK)
-        y_scale = keep.tile([P, QUERIES], U8, name="y_scale", align_bytes=64)
         words_out = out_1[0].rearrange("p q u -> p (q u)").bitcast(I32)
-
-        def gate(c, bank):
-            g = keep.tile([P, PACK, CHUNK], F32, name=f"gate{c}", tag=f"q_then_gate{c}", align_bytes=64)
-            nc.scalar.activation(g[:], bank[:], ACT.Silu)
-            return g
-
-        def multiply(c, g, bank):
-            y = keep.tile([P, PACK, CHUNK], F32, name=f"y{c}", tag={1: f"q_bf{CHUNK}", 2: "q_then_gate1"}.get(c, f"y{c}"), align_bytes=64)
-            nc.vector.tensor_tensor(y[:], bank[:], g[:], MULT)
-            nc.sync.dma_start(out_rows[:, :, c * CHUNK : (c + 1) * CHUNK], y[:])
-            return y
-
+        gates = keep.tile([P, PACK, QUERIES], F32, name="gates")
         y_bf = keep.tile([P, QUERIES * PACK], BF16, name="y_bf", align_bytes=64)
+        y_codes = keep.tile([P, QUERIES], U32, name="y_codes", align_bytes=64)
+        y_scale = keep.tile([P, QUERIES], U8, name="y_scale", align_bytes=64)
 
-        def round_y(c, y, copy):
-            dst = y_bf[:, c * CHUNK * PACK : (c + 1) * CHUNK * PACK].rearrange("p (c i t) -> p c t i", i=4, t=PACK)
-            copy(dst, y[:].rearrange("p t (c i) -> p c t i", i=4))
+        def multiply(y, bank, rows, lo, hi):
+            nc.vector.tensor_tensor(y[:, rows, :], bank[:], gates[:, rows, lo:hi], MULT)
+            nc.sync.dma_start(out_rows[:, rows, lo:hi], y[:, rows, :])
 
-        def quantise_y(y_codes, lo, hi):
+        def round_y(y, lo, width, copy):
+            dst = y_bf[:, lo * PACK : (lo + width) * PACK].rearrange("p (c i t) -> p c t i", i=4, t=PACK)
+            copy(dst, y.rearrange("p t (c i) -> p c t i", i=4))
+
+        def quantise_y(lo, hi):
             nc.vector.quantize_mx(y_codes[:, lo:hi].bitcast(FP8X4), y_scale[:, lo:hi], y_bf[:, lo * PACK : hi * PACK])
 
-        ksd = gather_scales(ks, "ks", lambda: quantise_q(round_q(q_first, 0, HALF), HALF, "scales_then_q0", 1))
+        THIRD, LAST = HALF, HALF + CHUNK
+        q_bf_third = keep.tile([P, CHUNK * PACK], BF16, name="q_bf_third", align_bytes=64)
+        q_bf_last = keep.tile([P, CHUNK * PACK], BF16, name="q_bf_last", tag="q_then_y", align_bytes=64)
+        q_bf_first = keep.tile([P, HALF * PACK], BF16, name="q_bf_first", align_bytes=64)
+        first = round_q(q_first[:], q_bf_first[:], nc.scalar.copy)
+        quantise_q(first, 0, HALF)
+        nc.vector.tensor_copy(k_plane[:].rearrange("p (r s) -> p r s", r=PACK), k_listed[:].rearrange("p (s r) -> p r s", r=PACK))
         kwd = gather_words(kw, "kw")
-        csd = gather_scales(cs, "cs", lambda: quantise_q(round_q(q_mid, 0, CHUNK), CHUNK, "scales_then_q1", 0))
+        a_first = {r: product(f"a_first{r}", kwd, k_plane, (r, r + 1), 0, HALF) for r in (0, 2)}
+        nc.scalar.activation(gates[:, 0:2, 0:HALF], a_first[0][:], ACT.Silu)
+        nc.scalar.activation(gates[:, 2:4, 0:HALF], a_first[2][:], ACT.Silu)
         cwd = gather_words(cw, "cw")
-        gates = {c: gate(c, product("a", kwd, ksd, 0, c)) for c in (1, 2)}
-        late = round_q(q_late, 0, CHUNK)
-        gates[0] = gate(0, product("a", kwd, ksd, 0, 0))
-        quantise_q(late, CHUNK, "words_then_q", 3)
-        z = {1: product("z", cwd, csd, 4, 1)}
-        gates[3] = gate(3, product("a", kwd, ksd, 0, 3))
-        for c in (0, 2, 3):
-            z[c] = product("z", cwd, csd, 4, c)
-        ys = {c: multiply(c, gates[c], z[c]) for c in (1, 0, 2, 3)}
-        for c in (1, 0, 2):
-            round_y(c, ys[c], nc.scalar.copy)
-        y_codes = keep.tile([P, QUERIES], U32, name="y_codes", tag="q_then_gate2", align_bytes=64)
-        quantise_y(y_codes, 0, 2 * CHUNK)
-        round_y(3, ys[3], nc.vector.tensor_copy)
-        quantise_y(y_codes, 2 * CHUNK, 3 * CHUNK)
-        nc.sync.dma_start(words_out[:, 0 : 3 * CHUNK], y_codes[:, 0 : 3 * CHUNK].bitcast(I32))
-        quantise_y(y_codes, 3 * CHUNK, 4 * CHUNK)
-        nc.sync.dma_start(words_out[:, 3 * CHUNK : QUERIES], y_codes[:, 3 * CHUNK : QUERIES].bitcast(I32))
+        third = round_q(q_third, q_bf_third[:], nc.scalar.copy)
+        last = round_q(q_last, q_bf_last[:], nc.vector.tensor_copy)
+        quantise_q(last, LAST, QUERIES)
+        quantise_q(third, THIRD, LAST)
+        z_first = {0: product("z_first0", cwd, c_plane, (0, 1), 0, HALF)}
+        a_last = product("a_last", kwd, k_plane, range(PACK), LAST, QUERIES)
+        a_third = product("a_third", kwd, k_plane, range(PACK), THIRD, LAST)
+        z_first[2] = product("z_first2", cwd, c_plane, (2, 3), 0, HALF)
+        nc.scalar.activation(gates[:, :, LAST:QUERIES], a_last[:], ACT.Silu)
+        nc.scalar.activation(gates[:, :, THIRD:LAST], a_third[:], ACT.Silu)
+        z_last = product("z_last", cwd, c_plane, range(PACK), LAST, QUERIES)
+        z_third = product("z_third", cwd, c_plane, range(PACK), THIRD, LAST)
+        y_first = keep.tile([P, PACK, HALF], F32, name="y_first", tag="q_then_y", align_bytes=64)
+        y_third = keep.tile([P, PACK, CHUNK], F32, name="y_third")
+        y_last = keep.tile([P, PACK, CHUNK], F32, name="y_last")
+        for r in (0, 2):
+            multiply(y_first, z_first[r], slice(r, r + 2), 0, HALF)
+        multiply(y_last, z_last, slice(0, PACK), LAST, QUERIES)
+        multiply(y_third, z_third, slice(0, PACK), THIRD, LAST)
+        round_y(y_first[:], 0, HALF, nc.scalar.copy)
+        round_y(y_last[:], LAST, CHUNK, nc.scalar.copy)
+        round_y(y_third[:], THIRD, CHUNK, nc.vector.tensor_copy)
+        quantise_y(0, HALF)
+        nc.sync.dma_start(words_out[:, 0:HALF], y_codes[:, 0:HALF].bitcast(I32))
+        quantise_y(THIRD, LAST)
+        quantise_y(LAST, QUERIES)
+        nc.sync.dma_start(words_out[:, HALF:QUERIES], y_codes[:, HALF:QUERIES].bitcast(I32))
         for quad in range(4):
             queue = nc.scalar if quad % 2 == 0 else nc.sync
             queue.dma_start(out_2[0, 4 * quad : 4 * quad + 4, :].bitcast(I32), y_scale[32 * quad : 32 * quad + 4, :].bitcast(I32))

@@ -32,9 +32,9 @@ def tile_attend_plh_swiglu_topk_kernel(tc, qT, k_words, k_scales, c_words, c_sca
         psum = ctx.enter_context(tc.psum_pool(name="psum", bufs=1))
 
         offsets = keep.tile([P, SLOTS // 16], U16, name="offsets")
-        kw = keep.tile([P, NEURONS], I32, name="kw")
+        kw = keep.tile([P, NEURONS], I32, name="kw", align_bytes=64)
         cw = keep.tile([P, NEURONS], I32, name="cw")
-        ks = keep.tile([P, NEURONS], U8, name="ks")
+        ks = keep.tile([P, NEURONS], U8, name="ks", align_bytes=64)
         cs = keep.tile([P, NEURONS], U8, name="cs")
         q_first = keep.tile([P, PACK, HALF], F32, name="q_first")
         q_rows = qT[0].rearrange("(p t) q -> p t q", t=PACK)
@@ -110,44 +110,61 @@ def tile_attend_plh_swiglu_topk_kernel(tc, qT, k_words, k_scales, c_words, c_sca
             nc.vector.quantize_mx(y_codes[:, lo:hi].bitcast(FP8X4), y_scale[:, lo:hi], y_bf[:, lo * PACK : hi * PACK])
 
         THIRD, LAST = HALF, HALF + CHUNK
-        q_bf_third = keep.tile([P, CHUNK * PACK], BF16, name="q_bf_third", align_bytes=64)
-        q_bf_last = keep.tile([P, CHUNK * PACK], BF16, name="q_bf_last", tag="q_then_y", align_bytes=64)
+        q_bf_third = keep.tile([P, CHUNK * PACK], BF16, name="q_bf_third", tag="q_then_y", align_bytes=64)
+        q_bf_last = keep.tile([P, CHUNK * PACK], BF16, name="q_bf_last", align_bytes=64)
         q_bf_first = keep.tile([P, HALF * PACK], BF16, name="q_bf_first", align_bytes=64)
         first = round_q(q_first[:], q_bf_first[:], nc.scalar.copy)
         quantise_q(first, 0, HALF)
         nc.vector.tensor_copy(k_plane[:].rearrange("p (r s) -> p r s", r=PACK), k_listed[:].rearrange("p (s r) -> p r s", r=PACK))
+        warm = psum.tile([P, SLOTS], F32, name="warm", tag="z_third")
+        for i in range(2):
+            nc.tensor.matmul_mx(
+                warm[:],
+                lhsT=kw[:, 0:P].bitcast(FP8X4),
+                lhsT_scale=ks[:, 0:P],
+                rhs=kw[:, 0:SLOTS].bitcast(FP8X4),
+                rhs_scale=ks[:, 0:SLOTS],
+                start=True,
+                stop=True,
+            )
         kwd = gather_words(kw, "kw")
         a_first = {r: product(f"a_first{r}", kwd, k_plane, (r, r + 1), 0, HALF) for r in (0, 2)}
         nc.scalar.activation(gates[:, 0:2, 0:HALF], a_first[0][:], ACT.Silu)
         nc.scalar.activation(gates[:, 2:4, 0:HALF], a_first[2][:], ACT.Silu)
         cwd = gather_words(cw, "cw")
-        third = round_q(q_third, q_bf_third[:], nc.scalar.copy)
-        last = round_q(q_last, q_bf_last[:], nc.vector.tensor_copy)
-        quantise_q(last, LAST, QUERIES)
-        quantise_q(third, THIRD, LAST)
-        z_first = {0: product("z_first0", cwd, c_plane, (0, 1), 0, HALF)}
-        a_last = product("a_last", kwd, k_plane, range(PACK), LAST, QUERIES)
+        round_q(q_third, q_bf_third[:], nc.vector.tensor_copy)
+        round_q(q_last, q_bf_last[:], nc.scalar.copy)
+        quantise_q(q_bf_third[:], THIRD, LAST)
+        quantise_q(q_bf_last[:], LAST, QUERIES)
+        row_groups = ((0,), (1,), (2, 3))
+        z_first = {rows: product(f"z_first{rows[0]}", cwd, c_plane, rows, 0, HALF) for rows in row_groups[:-1]}
         a_third = product("a_third", kwd, k_plane, range(PACK), THIRD, LAST)
-        z_first[2] = product("z_first2", cwd, c_plane, (2, 3), 0, HALF)
-        nc.scalar.activation(gates[:, :, LAST:QUERIES], a_last[:], ACT.Silu)
+        z_first[row_groups[-1]] = product("z_first2", cwd, c_plane, row_groups[-1], 0, HALF)
+        a_last = product("a_last", kwd, k_plane, range(PACK), LAST, QUERIES)
         nc.scalar.activation(gates[:, :, THIRD:LAST], a_third[:], ACT.Silu)
-        z_last = product("z_last", cwd, c_plane, range(PACK), LAST, QUERIES)
+        nc.scalar.activation(gates[:, :, LAST:QUERIES], a_last[:], ACT.Silu)
         z_third = product("z_third", cwd, c_plane, range(PACK), THIRD, LAST)
+        z_last = product("a_first0", cwd, c_plane, range(PACK), LAST, QUERIES)
         y_first = keep.tile([P, PACK, HALF], F32, name="y_first", tag="q_then_y", align_bytes=64)
         y_third = keep.tile([P, PACK, CHUNK], F32, name="y_third")
         y_last = keep.tile([P, PACK, CHUNK], F32, name="y_last")
-        for r in (0, 2):
-            multiply(y_first, z_first[r], slice(r, r + 2), 0, HALF)
-        multiply(y_last, z_last, slice(0, PACK), LAST, QUERIES)
+        for rows in row_groups:
+            part = slice(rows[0], rows[-1] + 1)
+            nc.vector.tensor_tensor(y_first[:, part, :], z_first[rows][:], gates[:, part, 0:HALF], MULT)
+            if rows[-1] % 2 == 1:
+                pair = slice(rows[-1] - 1, rows[-1] + 1)
+                nc.sync.dma_start(out_rows[:, pair, 0:HALF], y_first[:, pair, :])
         multiply(y_third, z_third, slice(0, PACK), THIRD, LAST)
-        round_y(y_first[:], 0, HALF, nc.scalar.copy)
-        round_y(y_last[:], LAST, CHUNK, nc.scalar.copy)
-        round_y(y_third[:], THIRD, CHUNK, nc.vector.tensor_copy)
+        multiply(y_last, z_last, slice(0, PACK), LAST, QUERIES)
+        nc.gpsimd.tensor_copy(y_bf[:, 0 : CHUNK * PACK].rearrange("p (q t) -> p q t", t=PACK), y_first[:, :, 0:CHUNK].rearrange("p t q -> p q t"))
+        round_y(y_first[:, :, CHUNK:HALF], CHUNK, CHUNK, nc.scalar.copy)
+        round_y(y_third[:], THIRD, CHUNK, nc.scalar.copy)
         quantise_y(0, HALF)
-        nc.sync.dma_start(words_out[:, 0:HALF], y_codes[:, 0:HALF].bitcast(I32))
+        round_y(y_last[:], LAST, CHUNK, nc.vector.tensor_copy)
         quantise_y(THIRD, LAST)
+        nc.sync.dma_start(words_out[:, 0:LAST], y_codes[:, 0:LAST].bitcast(I32))
         quantise_y(LAST, QUERIES)
-        nc.sync.dma_start(words_out[:, HALF:QUERIES], y_codes[:, HALF:QUERIES].bitcast(I32))
+        nc.sync.dma_start(words_out[:, LAST:QUERIES], y_codes[:, LAST:QUERIES].bitcast(I32))
         for quad in range(4):
             queue = nc.scalar if quad % 2 == 0 else nc.sync
             queue.dma_start(out_2[0, 4 * quad : 4 * quad + 4, :].bitcast(I32), y_scale[32 * quad : 32 * quad + 4, :].bitcast(I32))

@@ -11,6 +11,7 @@ U8 = mybir.dt.uint8
 FP8X4 = mybir.dt.float8_e4m3fn_x4
 ACT = mybir.ActivationFunctionType
 MULT = mybir.AluOpType.mult
+ADD = mybir.AluOpType.add
 
 P = 128
 PACK = 4
@@ -156,11 +157,12 @@ def tile_attend_plh_swiglu_topk_kernel(tc, qT, k_words, k_scales, c_words, c_sca
                 nc.sync.dma_start(out_rows[:, pair, 0:HALF], y_first[:, pair, :])
         multiply(y_third, z_third, slice(0, PACK), THIRD, LAST)
         multiply(y_last, z_last, slice(0, PACK), LAST, QUERIES)
-        nc.gpsimd.tensor_copy(y_bf[:, 0 : CHUNK * PACK].rearrange("p (q t) -> p q t", t=PACK), y_first[:, :, 0:CHUNK].rearrange("p t q -> p q t"))
+        nc.gpsimd.tensor_scalar(y_bf[:, 0 : CHUNK * PACK].rearrange("p (q t) -> p q t", t=PACK), y_first[:, :, 0:CHUNK].rearrange("p t q -> p q t"), 1.0, -0.0, MULT, ADD)
         round_y(y_first[:, :, CHUNK:HALF], CHUNK, CHUNK, nc.scalar.copy)
         round_y(y_third[:], THIRD, CHUNK, nc.scalar.copy)
         quantise_y(0, HALF)
-        round_y(y_last[:], LAST, CHUNK, nc.vector.tensor_copy)
+        round_y(y_last[:, :, 0:64], LAST, 64, nc.scalar.copy)
+        round_y(y_last[:, :, 64:CHUNK], LAST + 64, CHUNK - 64, nc.vector.tensor_copy)
         quantise_y(THIRD, LAST)
         nc.sync.dma_start(words_out[:, 0:LAST], y_codes[:, 0:LAST].bitcast(I32))
         quantise_y(LAST, QUERIES)

@@ -15,13 +15,19 @@ ADD = mybir.AluOpType.add
 
 P = 128
 PACK = 4
+QUADS = 4
 SLOTS = 512
 NEURONS = 2048
 QUERIES = 512
+BLOCKS = 16
+COMPACT = P - BLOCKS
 CHUNK = 128
 HALF = 256
-BLOCKS = 16
-ROW0 = P - BLOCKS
+THIRD = HALF
+LAST = HALF + CHUNK
+LAST_Q_ON_VECTOR = 32
+LAST_Y_ON_SCALAR = 64
+WARM_UPS = 2
 
 FLOPS = 2 * 2 * 512 * 512 * 512
 
@@ -41,42 +47,57 @@ def tile_attend_plh_swiglu_topk_kernel(tc, qT, k_words, k_scales, c_words, c_sca
         q_rows = qT[0].rearrange("(p t) q -> p t q", t=PACK)
 
         nc.vector.memset(ks[:].bitcast(I32), 0)
-        nc.vector.memset(cs[0:ROW0, :].bitcast(I32), 0)
+        nc.vector.memset(cs[0:COMPACT, :].bitcast(I32), 0)
         nc.sync.dma_start(offsets[:], offs)
-        nc.sync.dma_start(cs[ROW0:P, :].bitcast(I32), c_scales[0].bitcast(I32))
+        nc.scalar.dma_start(cs[COMPACT:P, :].bitcast(I32), c_scales[0].bitcast(I32))
         nc.sync.dma_start(q_first[:], q_rows[:, :, 0:HALF])
-        for i in range(4):
-            nc.sync.dma_start(ks[i:P:32, :].bitcast(I32), k_scales[0, i:16:4, :].bitcast(I32))
+        for i in range(BLOCKS // QUADS):
+            nc.sync.dma_start(ks[i:P:32, :].bitcast(I32), k_scales[0, i:BLOCKS:QUADS, :].bitcast(I32))
         nc.sync.dma_start(kw[:], k_words[0].rearrange("p n t -> p (n t)").bitcast(I32))
         nc.sync.dma_start(cw[:], c_words[0].rearrange("p n t -> p (n t)").bitcast(I32))
+
+        def deal_scales(plane, listed):
+            nc.vector.tensor_copy(plane[:].rearrange("p (r s) -> p r s", r=PACK), listed[:].rearrange("p (s r) -> p r s", r=PACK))
+
+        def gather_words(table, name):
+            dealt = keep.tile([P, SLOTS], U32, name=name, align_bytes=64)
+            nc.vector.tensor_copy(dealt[:].rearrange("p (r s) -> p s r", r=PACK), table[:].bitcast(U32).indirect(offsets[:]))
+            return dealt
 
         k_listed = keep.tile([P, SLOTS], U8, name="k_listed")
         c_listed = keep.tile([P, SLOTS], U8, name="c_listed", tag="listed_then_q")
         k_plane = keep.tile([P, SLOTS], U8, name="k_plane", align_bytes=64)
         c_plane = keep.tile([P, SLOTS], U8, name="c_plane", align_bytes=64)
         nc.vector.tensor_copy(c_listed[:], cs[:].indirect(offsets[:]))
-        nc.vector.tensor_copy(c_plane[:].rearrange("p (r s) -> p r s", r=PACK), c_listed[:].rearrange("p (s r) -> p r s", r=PACK))
-        for quad in range(4):
-            nc.sync.dma_start(c_plane[32 * quad : 32 * quad + 4, :].bitcast(I32), c_plane[ROW0 + 4 * quad : ROW0 + 4 * quad + 4, :].bitcast(I32))
+        deal_scales(c_plane, c_listed)
+        for quad in range(QUADS):
+            src = COMPACT + 4 * quad
+            nc.sync.dma_start(c_plane[32 * quad : 32 * quad + 4, :].bitcast(I32), c_plane[src : src + 4, :].bitcast(I32))
         q_late = keep.tile([P, PACK, HALF], F32, name="q_late", tag="listed_then_q")
-        q_third, q_last = q_late[:, :, 0:CHUNK], q_late[:, :, CHUNK:HALF]
         nc.sync.dma_start(q_late[:], q_rows[:, :, HALF:QUERIES])
         nc.vector.tensor_copy(k_listed[:], ks[:].indirect(offsets[:]))
 
-        def gather_words(table, name):
-            dealt = keep.tile([P, SLOTS], U32, name=name + "_dealt", align_bytes=64)
-            nc.vector.tensor_copy(dealt[:].rearrange("p (r s) -> p s r", r=PACK), table[:].bitcast(U32).indirect(offsets[:]))
-            return dealt
-
         q_codes = keep.tile([P, QUERIES], U32, name="q_codes", align_bytes=64)
         q_scale = keep.tile([P, QUERIES], U8, name="q_scale", align_bytes=64)
+        gates = keep.tile([P, PACK, QUERIES], F32, name="gates")
+        y_bf = keep.tile([P, QUERIES * PACK], BF16, name="y_bf", align_bytes=64)
+        y_codes = keep.tile([P, QUERIES], U32, name="y_codes", align_bytes=64)
+        y_scale = keep.tile([P, QUERIES], U8, name="y_scale", align_bytes=64)
+        q_bf_third = keep.tile([P, CHUNK * PACK], BF16, name="q_bf_third", tag="q_then_y", align_bytes=64)
+        q_bf_last = keep.tile([P, CHUNK * PACK], BF16, name="q_bf_last", align_bytes=64)
+        q_bf_first = keep.tile([P, HALF * PACK], BF16, name="q_bf_first", align_bytes=64)
+        out_rows = out_0.rearrange("(p r) q -> p r q", r=PACK)
+        words_out = out_1[0].rearrange("p q u -> p (q u)").bitcast(I32)
 
-        def round_q(raw, q_bf, copy):
-            copy(q_bf.rearrange("p (c i t) -> p c t i", i=4, t=PACK), raw.rearrange("p t (c i) -> p c t i", i=4))
-            return q_bf
+        def round_to_words(copy, dst, lo, src):
+            part = dst[:, lo * PACK : (lo + src.shape[2]) * PACK]
+            copy(part.rearrange("p (c i t) -> p c t i", i=4, t=PACK), src.rearrange("p t (c i) -> p c t i", i=4))
 
         def quantise_q(q_bf, lo, hi):
-            nc.vector.quantize_mx(q_codes[:, lo:hi].bitcast(FP8X4), q_scale[:, lo:hi], q_bf)
+            nc.vector.quantize_mx(q_codes[:, lo:hi].bitcast(FP8X4), q_scale[:, lo:hi], q_bf[:])
+
+        def quantise_y(lo, hi):
+            nc.vector.quantize_mx(y_codes[:, lo:hi].bitcast(FP8X4), y_scale[:, lo:hi], y_bf[:, lo * PACK : hi * PACK])
 
         def product(name, words, plane, rows, lo, hi):
             bank = psum.tile([P, len(rows), hi - lo], F32, name=name)
@@ -92,33 +113,16 @@ def tile_attend_plh_swiglu_topk_kernel(tc, qT, k_words, k_scales, c_words, c_sca
                 )
             return bank
 
-        out_rows = out_0.rearrange("(p r) q -> p r q", r=PACK)
-        words_out = out_1[0].rearrange("p q u -> p (q u)").bitcast(I32)
-        gates = keep.tile([P, PACK, QUERIES], F32, name="gates")
-        y_bf = keep.tile([P, QUERIES * PACK], BF16, name="y_bf", align_bytes=64)
-        y_codes = keep.tile([P, QUERIES], U32, name="y_codes", align_bytes=64)
-        y_scale = keep.tile([P, QUERIES], U8, name="y_scale", align_bytes=64)
-
         def multiply(y, bank, rows, lo, hi):
             nc.vector.tensor_tensor(y[:, rows, :], bank[:], gates[:, rows, lo:hi], MULT)
             nc.sync.dma_start(out_rows[:, rows, lo:hi], y[:, rows, :])
 
-        def round_y(y, lo, width, copy):
-            dst = y_bf[:, lo * PACK : (lo + width) * PACK].rearrange("p (c i t) -> p c t i", i=4, t=PACK)
-            copy(dst, y.rearrange("p t (c i) -> p c t i", i=4))
+        round_to_words(nc.scalar.copy, q_bf_first, 0, q_first[:])
+        quantise_q(q_bf_first, 0, HALF)
+        deal_scales(k_plane, k_listed)
 
-        def quantise_y(lo, hi):
-            nc.vector.quantize_mx(y_codes[:, lo:hi].bitcast(FP8X4), y_scale[:, lo:hi], y_bf[:, lo * PACK : hi * PACK])
-
-        THIRD, LAST = HALF, HALF + CHUNK
-        q_bf_third = keep.tile([P, CHUNK * PACK], BF16, name="q_bf_third", tag="q_then_y", align_bytes=64)
-        q_bf_last = keep.tile([P, CHUNK * PACK], BF16, name="q_bf_last", align_bytes=64)
-        q_bf_first = keep.tile([P, HALF * PACK], BF16, name="q_bf_first", align_bytes=64)
-        first = round_q(q_first[:], q_bf_first[:], nc.scalar.copy)
-        quantise_q(first, 0, HALF)
-        nc.vector.tensor_copy(k_plane[:].rearrange("p (r s) -> p r s", r=PACK), k_listed[:].rearrange("p (s r) -> p r s", r=PACK))
         warm = psum.tile([P, SLOTS], F32, name="warm", tag="z_third")
-        for i in range(2):
+        for i in range(WARM_UPS):
             nc.tensor.matmul_mx(
                 warm[:],
                 lhsT=kw[:, 0:P].bitcast(FP8X4),
@@ -128,45 +132,53 @@ def tile_attend_plh_swiglu_topk_kernel(tc, qT, k_words, k_scales, c_words, c_sca
                 start=True,
                 stop=True,
             )
-        kwd = gather_words(kw, "kw")
-        a_first = {r: product(f"a_first{r}", kwd, k_plane, (r, r + 1), 0, HALF) for r in (0, 2)}
-        nc.scalar.activation(gates[:, 0:2, 0:HALF], a_first[0][:], ACT.Silu)
-        nc.scalar.activation(gates[:, 2:4, 0:HALF], a_first[2][:], ACT.Silu)
-        cwd = gather_words(cw, "cw")
-        round_q(q_third, q_bf_third[:], nc.vector.tensor_copy)
-        round_q(q_last, q_bf_last[:], nc.scalar.copy)
-        quantise_q(q_bf_third[:], THIRD, LAST)
-        quantise_q(q_bf_last[:], LAST, QUERIES)
-        row_groups = ((0,), (1,), (2, 3))
-        z_first = {rows: product(f"z_first{rows[0]}", cwd, c_plane, rows, 0, HALF) for rows in row_groups[:-1]}
-        a_third = product("a_third", kwd, k_plane, range(PACK), THIRD, LAST)
-        z_first[row_groups[-1]] = product("z_first2", cwd, c_plane, row_groups[-1], 0, HALF)
-        a_last = product("a_last", kwd, k_plane, range(PACK), LAST, QUERIES)
+
+        k_dealt = gather_words(kw, "k_dealt")
+        a_first = {r: product(f"a_first{r}", k_dealt, k_plane, (r, r + 1), 0, HALF) for r in (0, 2)}
+        for r in (0, 2):
+            nc.scalar.activation(gates[:, r : r + 2, 0:HALF], a_first[r][:], ACT.Silu)
+        c_dealt = gather_words(cw, "c_dealt")
+
+        round_to_words(nc.vector.tensor_copy, q_bf_third, 0, q_late[:, :, 0:CHUNK])
+        round_to_words(nc.vector.tensor_copy, q_bf_last, 0, q_late[:, :, CHUNK : CHUNK + LAST_Q_ON_VECTOR])
+        round_to_words(nc.scalar.copy, q_bf_last, LAST_Q_ON_VECTOR, q_late[:, :, CHUNK + LAST_Q_ON_VECTOR : HALF])
+        quantise_q(q_bf_third, THIRD, LAST)
+        quantise_q(q_bf_last, LAST, QUERIES)
+
+        z_first = {0: product("z_first0", c_dealt, c_plane, (0, 1), 0, HALF)}
+        a_third = product("a_third", k_dealt, k_plane, range(PACK), THIRD, LAST)
+        z_first[2] = product("z_first2", c_dealt, c_plane, (2, 3), 0, HALF)
+        a_last = product("a_last", k_dealt, k_plane, range(PACK), LAST, QUERIES)
         nc.scalar.activation(gates[:, :, THIRD:LAST], a_third[:], ACT.Silu)
         nc.scalar.activation(gates[:, :, LAST:QUERIES], a_last[:], ACT.Silu)
-        z_third = product("z_third", cwd, c_plane, range(PACK), THIRD, LAST)
-        z_last = product("a_first0", cwd, c_plane, range(PACK), LAST, QUERIES)
+        z_third = product("z_third", c_dealt, c_plane, range(PACK), THIRD, LAST)
+        z_last = product("z_last", c_dealt, c_plane, range(PACK), LAST, QUERIES)
+
         y_first = keep.tile([P, PACK, HALF], F32, name="y_first", tag="q_then_y", align_bytes=64)
         y_third = keep.tile([P, PACK, CHUNK], F32, name="y_third")
         y_last = keep.tile([P, PACK, CHUNK], F32, name="y_last")
-        for rows in row_groups:
-            part = slice(rows[0], rows[-1] + 1)
-            nc.vector.tensor_tensor(y_first[:, part, :], z_first[rows][:], gates[:, part, 0:HALF], MULT)
-            if rows[-1] % 2 == 1:
-                pair = slice(rows[-1] - 1, rows[-1] + 1)
-                nc.sync.dma_start(out_rows[:, pair, 0:HALF], y_first[:, pair, :])
+        for r in (0, 2):
+            multiply(y_first, z_first[r], slice(r, r + 2), 0, HALF)
         multiply(y_third, z_third, slice(0, PACK), THIRD, LAST)
         multiply(y_last, z_last, slice(0, PACK), LAST, QUERIES)
-        nc.gpsimd.tensor_scalar(y_bf[:, 0 : CHUNK * PACK].rearrange("p (q t) -> p q t", t=PACK), y_first[:, :, 0:CHUNK].rearrange("p t q -> p q t"), 1.0, -0.0, MULT, ADD)
-        round_y(y_first[:, :, CHUNK:HALF], CHUNK, CHUNK, nc.scalar.copy)
-        round_y(y_third[:], THIRD, CHUNK, nc.scalar.copy)
+
+        nc.gpsimd.tensor_scalar(
+            y_bf[:, 0 : CHUNK * PACK].rearrange("p (q t) -> p q t", t=PACK),
+            y_first[:, :, 0:CHUNK].rearrange("p t q -> p q t"),
+            1.0,
+            -0.0,
+            MULT,
+            ADD,
+        )
+        round_to_words(nc.scalar.copy, y_bf, CHUNK, y_first[:, :, CHUNK:HALF])
+        round_to_words(nc.scalar.copy, y_bf, THIRD, y_third[:])
         quantise_y(0, HALF)
-        round_y(y_last[:, :, 0:64], LAST, 64, nc.scalar.copy)
-        round_y(y_last[:, :, 64:CHUNK], LAST + 64, CHUNK - 64, nc.vector.tensor_copy)
+        round_to_words(nc.scalar.copy, y_bf, LAST, y_last[:, :, 0:LAST_Y_ON_SCALAR])
+        round_to_words(nc.vector.tensor_copy, y_bf, LAST + LAST_Y_ON_SCALAR, y_last[:, :, LAST_Y_ON_SCALAR:CHUNK])
         quantise_y(THIRD, LAST)
         nc.sync.dma_start(words_out[:, 0:LAST], y_codes[:, 0:LAST].bitcast(I32))
         quantise_y(LAST, QUERIES)
         nc.sync.dma_start(words_out[:, LAST:QUERIES], y_codes[:, LAST:QUERIES].bitcast(I32))
-        for quad in range(4):
+        for quad in range(QUADS):
             queue = nc.scalar if quad % 2 == 0 else nc.sync
             queue.dma_start(out_2[0, 4 * quad : 4 * quad + 4, :].bitcast(I32), y_scale[32 * quad : 32 * quad + 4, :].bitcast(I32))

@@ -114,7 +114,7 @@ def tile_attend_plh_swiglu_topk_kernel(tc, qT, k_words, k_scales, c_words, c_sca
             return bank
 
         def multiply(y, bank, rows, lo, hi):
-            nc.vector.tensor_tensor(y[:, rows, :], bank[:], gates[:, rows, lo:hi], MULT)
+            nc.vector.tensor_tensor(y[:, rows, :], bank, gates[:, rows, lo:hi], MULT)
             nc.sync.dma_start(out_rows[:, rows, lo:hi], y[:, rows, :])
 
         round_to_words(nc.scalar.copy, q_bf_first, 0, q_first[:])
@@ -157,10 +157,10 @@ def tile_attend_plh_swiglu_topk_kernel(tc, qT, k_words, k_scales, c_words, c_sca
         y_first = keep.tile([P, PACK, HALF], F32, name="y_first", tag="q_then_y", align_bytes=64)
         y_third = keep.tile([P, PACK, CHUNK], F32, name="y_third")
         y_last = keep.tile([P, PACK, CHUNK], F32, name="y_last")
-        for r in (0, 2):
-            multiply(y_first, z_first[r], slice(r, r + 2), 0, HALF)
-        multiply(y_third, z_third, slice(0, PACK), THIRD, LAST)
-        multiply(y_last, z_last, slice(0, PACK), LAST, QUERIES)
+        for r in range(PACK):
+            multiply(y_first, z_first[r - r % 2][:, r % 2 : r % 2 + 1, :], slice(r, r + 1), 0, HALF)
+        multiply(y_third, z_third[:], slice(0, PACK), THIRD, LAST)
+        multiply(y_last, z_last[:], slice(0, PACK), LAST, QUERIES)
 
         nc.gpsimd.tensor_scalar(
             y_bf[:, 0 : CHUNK * PACK].rearrange("p (q t) -> p q t", t=PACK),
@@ -176,9 +176,8 @@ def tile_attend_plh_swiglu_topk_kernel(tc, qT, k_words, k_scales, c_words, c_sca
         round_to_words(nc.scalar.copy, y_bf, LAST, y_last[:, :, 0:LAST_Y_ON_SCALAR])
         round_to_words(nc.vector.tensor_copy, y_bf, LAST + LAST_Y_ON_SCALAR, y_last[:, :, LAST_Y_ON_SCALAR:CHUNK])
         quantise_y(THIRD, LAST)
-        nc.sync.dma_start(words_out[:, 0:LAST], y_codes[:, 0:LAST].bitcast(I32))
         quantise_y(LAST, QUERIES)
-        nc.sync.dma_start(words_out[:, LAST:QUERIES], y_codes[:, LAST:QUERIES].bitcast(I32))
+        nc.sync.dma_start(words_out, y_codes[:].bitcast(I32))
         for quad in range(QUADS):
             queue = nc.scalar if quad % 2 == 0 else nc.sync
             queue.dma_start(out_2[0, 4 * quad : 4 * quad + 4, :].bitcast(I32), y_scale[32 * quad : 32 * quad + 4, :].bitcast(I32))

@@ -121,20 +121,19 @@ def tile_attend_plh_swiglu_topk_kernel(tc, qT, k_words, k_scales, c_words, c_sca
         quantise_q(q_bf_first, 0, HALF)
         deal_scales(k_plane, k_listed)
 
+        k_dealt = gather_words(kw, "k_dealt")
+        a_first = {r: product(f"a_first{r}", k_dealt, k_plane, (r, r + 1), 0, HALF) for r in (0, 2)}
         warm = psum.tile([P, SLOTS], F32, name="warm", tag="z_third")
         for i in range(WARM_UPS):
             nc.tensor.matmul_mx(
                 warm[:],
-                lhsT=kw[:, 0:P].bitcast(FP8X4),
-                lhsT_scale=ks[:, 0:P],
-                rhs=kw[:, 0:SLOTS].bitcast(FP8X4),
-                rhs_scale=ks[:, 0:SLOTS],
+                lhsT=q_codes[:, 0:P].bitcast(FP8X4),
+                lhsT_scale=q_scale[:, 0:P],
+                rhs=k_dealt[:].bitcast(FP8X4),
+                rhs_scale=k_plane[:],
                 start=True,
                 stop=True,
             )
-
-        k_dealt = gather_words(kw, "k_dealt")
-        a_first = {r: product(f"a_first{r}", k_dealt, k_plane, (r, r + 1), 0, HALF) for r in (0, 2)}
         for r in (0, 2):
             nc.scalar.activation(gates[:, r : r + 2, 0:HALF], a_first[r][:], ACT.Silu)
         c_dealt = gather_words(cw, "c_dealt")

@@ -27,7 +27,6 @@ THIRD = HALF
 LAST = HALF + CHUNK
 LAST_Q_ON_VECTOR = 32
 LAST_Y_ON_SCALAR = 64
-WARM_UPS = 2
 
 FLOPS = 2 * 2 * 512 * 512 * 512
 
@@ -123,17 +122,6 @@ def tile_attend_plh_swiglu_topk_kernel(tc, qT, k_words, k_scales, c_words, c_sca
 
         k_dealt = gather_words(kw, "k_dealt")
         a_first = {r: product(f"a_first{r}", k_dealt, k_plane, (r, r + 1), 0, HALF) for r in (0, 2)}
-        warm = psum.tile([P, SLOTS], F32, name="warm", tag="z_third")
-        for i in range(WARM_UPS):
-            nc.tensor.matmul_mx(
-                warm[:],
-                lhsT=q_codes[:, 0:P].bitcast(FP8X4),
-                lhsT_scale=q_scale[:, 0:P],
-                rhs=k_dealt[:].bitcast(FP8X4),
-                rhs_scale=k_plane[:],
-                start=True,
-                stop=True,
-            )
         for r in (0, 2):
             nc.scalar.activation(gates[:, r : r + 2, 0:HALF], a_first[r][:], ACT.Silu)
         c_dealt = gather_words(cw, "c_dealt")

@@ -122,6 +122,17 @@ def tile_attend_plh_swiglu_topk_kernel(tc, qT, k_words, k_scales, c_words, c_sca
 
         k_dealt = gather_words(kw, "k_dealt")
         a_first = {r: product(f"a_first{r}", k_dealt, k_plane, (r, r + 1), 0, HALF) for r in (0, 2)}
+        warm = psum.tile([P, LAST], F32, name="warm", tag="z_last")
+        for start, width in ((0, HALF), (HALF, CHUNK)):
+            nc.tensor.matmul_mx(
+                warm[:, start : start + width],
+                lhsT=k_dealt[:, 0:P].bitcast(FP8X4),
+                lhsT_scale=k_plane[:, 0:P],
+                rhs=q_codes[:, 0:width].bitcast(FP8X4),
+                rhs_scale=q_scale[:, 0:width],
+                start=True,
+                stop=True,
+            )
         for r in (0, 2):
             nc.scalar.activation(gates[:, r : r + 2, 0:HALF], a_first[r][:], ACT.Silu)
         c_dealt = gather_words(cw, "c_dealt")

@@ -41,7 +41,7 @@ def tile_attend_plh_swiglu_topk_kernel(tc, qT, k_words, k_scales, c_words, c_sca
         kw = keep.tile([P, NEURONS], I32, name="kw", align_bytes=64)
         cw = keep.tile([P, NEURONS], I32, name="cw")
         ks = keep.tile([P, NEURONS], U8, name="ks", align_bytes=64)
-        cs = keep.tile([P, NEURONS], U8, name="cs")
+        cs = keep.tile([P, NEURONS], U8, name="cs", tag="cs_then_q")
         q_first = keep.tile([P, PACK, HALF], F32, name="q_first")
         q_rows = qT[0].rearrange("(p t) q -> p t q", t=PACK)
 
@@ -55,26 +55,20 @@ def tile_attend_plh_swiglu_topk_kernel(tc, qT, k_words, k_scales, c_words, c_sca
         nc.sync.dma_start(kw[:], k_words[0].rearrange("p n t -> p (n t)").bitcast(I32))
         nc.sync.dma_start(cw[:], c_words[0].rearrange("p n t -> p (n t)").bitcast(I32))
 
-        def deal_scales(plane, listed):
-            nc.vector.tensor_copy(plane[:].rearrange("p (r s) -> p r s", r=PACK), listed[:].rearrange("p (s r) -> p r s", r=PACK))
-
-        def gather_words(table, name):
-            dealt = keep.tile([P, SLOTS], U32, name=name, align_bytes=64)
-            nc.vector.tensor_copy(dealt[:].rearrange("p (r s) -> p s r", r=PACK), table[:].bitcast(U32).indirect(offsets[:]))
+        def gather_dealt(table, dtype, name):
+            dealt = keep.tile([P, SLOTS], dtype, name=name, align_bytes=64)
+            nc.vector.tensor_copy(dealt[:].rearrange("p (r s) -> p s r", r=PACK), table[:].bitcast(dtype).indirect(offsets[:]))
             return dealt
 
-        k_listed = keep.tile([P, SLOTS], U8, name="k_listed")
-        c_listed = keep.tile([P, SLOTS], U8, name="c_listed", tag="listed_then_q")
-        k_plane = keep.tile([P, SLOTS], U8, name="k_plane", align_bytes=64)
         c_plane = keep.tile([P, SLOTS], U8, name="c_plane", align_bytes=64)
-        nc.vector.tensor_copy(c_listed[:], cs[:].indirect(offsets[:]))
-        deal_scales(c_plane, c_listed)
+        nc.vector.memset(c_plane[:].bitcast(I32), 0)
+        c_compact = gather_dealt(cs, U8, "c_compact")
         for quad in range(QUADS):
             src = COMPACT + 4 * quad
-            nc.sync.dma_start(c_plane[32 * quad : 32 * quad + 4, :].bitcast(I32), c_plane[src : src + 4, :].bitcast(I32))
-        q_late = keep.tile([P, PACK, HALF], F32, name="q_late", tag="listed_then_q")
+            nc.sync.dma_start(c_plane[32 * quad : 32 * quad + 4, :].bitcast(I32), c_compact[src : src + 4, :].bitcast(I32))
+        q_late = keep.tile([P, PACK, HALF], F32, name="q_late", tag="cs_then_q")
         nc.sync.dma_start(q_late[:], q_rows[:, :, HALF:QUERIES])
-        nc.vector.tensor_copy(k_listed[:], ks[:].indirect(offsets[:]))
+        k_plane = gather_dealt(ks, U8, "k_plane")
 
         q_codes = keep.tile([P, QUERIES], U32, name="q_codes", align_bytes=64)
         q_scale = keep.tile([P, QUERIES], U8, name="q_scale", align_bytes=64)
@@ -118,9 +112,8 @@ def tile_attend_plh_swiglu_topk_kernel(tc, qT, k_words, k_scales, c_words, c_sca
 
         round_to_words(nc.scalar.copy, q_bf_first, 0, q_first[:])
         quantise_q(q_bf_first, 0, HALF)
-        deal_scales(k_plane, k_listed)
 
-        k_dealt = gather_words(kw, "k_dealt")
+        k_dealt = gather_dealt(kw, U32, "k_dealt")
         a_first = {r: product(f"a_first{r}", k_dealt, k_plane, (r, r + 1), 0, HALF) for r in (0, 2)}
         warm = psum.tile([P, LAST], F32, name="warm", tag="z_last")
         for start, width in ((0, HALF), (HALF, CHUNK)):
@@ -135,7 +128,7 @@ def tile_attend_plh_swiglu_topk_kernel(tc, qT, k_words, k_scales, c_words, c_sca
             )
         for r in (0, 2):
             nc.scalar.activation(gates[:, r : r + 2, 0:HALF], a_first[r][:], ACT.Silu)
-        c_dealt = gather_words(cw, "c_dealt")
+        c_dealt = gather_dealt(cw, U32, "c_dealt")
 
         round_to_words(nc.vector.tensor_copy, q_bf_third, 0, q_late[:, :, 0:CHUNK])
         round_to_words(nc.vector.tensor_copy, q_bf_last, 0, q_late[:, :, CHUNK : CHUNK + LAST_Q_ON_VECTOR])

@@ -72,7 +72,6 @@ def tile_attend_plh_swiglu_topk_kernel(tc, qT, k_words, k_scales, c_words, c_sca
 
         q_codes = keep.tile([P, QUERIES], U32, name="q_codes", align_bytes=64)
         q_scale = keep.tile([P, QUERIES], U8, name="q_scale", align_bytes=64)
-        gates = keep.tile([P, PACK, QUERIES], F32, name="gates")
         y_bf = keep.tile([P, QUERIES * PACK], BF16, name="y_bf", align_bytes=64)
         y_codes = keep.tile([P, QUERIES], U32, name="y_codes", align_bytes=64)
         y_scale = keep.tile([P, QUERIES], U8, name="y_scale", align_bytes=64)
@@ -106,8 +105,13 @@ def tile_attend_plh_swiglu_topk_kernel(tc, qT, k_words, k_scales, c_words, c_sca
                 )
             return bank
 
-        def multiply(y, bank, rows, lo, hi):
-            nc.vector.tensor_tensor(y[:, rows, :], bank, gates[:, rows, lo:hi], MULT)
+        def gate(bank, name, tag=""):
+            gates = keep.tile(list(bank.shape), F32, name=name, tag=tag)
+            nc.scalar.activation(gates[:], bank[:], ACT.Silu)
+            return gates
+
+        def multiply(y, bank, gates, rows, lo, hi):
+            nc.vector.tensor_tensor(y[:, rows, :], bank, gates, MULT)
             nc.sync.dma_start(out_rows[:, rows, lo:hi], y[:, rows, :])
 
         round_to_words(nc.scalar.copy, q_bf_first, 0, q_first[:])
@@ -126,13 +130,13 @@ def tile_attend_plh_swiglu_topk_kernel(tc, qT, k_words, k_scales, c_words, c_sca
                 start=True,
                 stop=True,
             )
-        for r in (0, 2):
-            nc.scalar.activation(gates[:, r : r + 2, 0:HALF], a_first[r][:], ACT.Silu)
+        g_first = {0: gate(a_first[0], "g_first0")}
         c_dealt = gather_dealt(cw, U32, "c_dealt")
 
         round_to_words(nc.vector.tensor_copy, q_bf_third, 0, q_late[:, :, 0:CHUNK])
         round_to_words(nc.vector.tensor_copy, q_bf_last, 0, q_late[:, :, CHUNK : CHUNK + LAST_Q_ON_VECTOR])
         round_to_words(nc.scalar.copy, q_bf_last, LAST_Q_ON_VECTOR, q_late[:, :, CHUNK + LAST_Q_ON_VECTOR : HALF])
+        g_first[2] = gate(a_first[2], "g_first2", tag="cs_then_q")
         quantise_q(q_bf_third, THIRD, LAST)
         quantise_q(q_bf_last, LAST, QUERIES)
 
@@ -140,8 +144,8 @@ def tile_attend_plh_swiglu_topk_kernel(tc, qT, k_words, k_scales, c_words, c_sca
         a_third = product("a_third", k_dealt, k_plane, range(PACK), THIRD, LAST)
         z_first[2] = product("z_first2", c_dealt, c_plane, (2, 3), 0, HALF)
         a_last = product("a_last", k_dealt, k_plane, range(PACK), LAST, QUERIES)
-        nc.scalar.activation(gates[:, :, THIRD:LAST], a_third[:], ACT.Silu)
-        nc.scalar.activation(gates[:, :, LAST:QUERIES], a_last[:], ACT.Silu)
+        g_third = gate(a_third, "g_third")
+        g_last = gate(a_last, "g_last")
         z_third = product("z_third", c_dealt, c_plane, range(PACK), THIRD, LAST)
         z_last = product("z_last", c_dealt, c_plane, range(PACK), LAST, QUERIES)
 
@@ -149,9 +153,10 @@ def tile_attend_plh_swiglu_topk_kernel(tc, qT, k_words, k_scales, c_words, c_sca
         y_third = keep.tile([P, PACK, CHUNK], F32, name="y_third")
         y_last = keep.tile([P, PACK, CHUNK], F32, name="y_last")
         for r in range(PACK):
-            multiply(y_first, z_first[r - r % 2][:, r % 2 : r % 2 + 1, :], slice(r, r + 1), 0, HALF)
-        multiply(y_third, z_third[:], slice(0, PACK), THIRD, LAST)
-        multiply(y_last, z_last[:], slice(0, PACK), LAST, QUERIES)
+            pair, row = r - r % 2, slice(r % 2, r % 2 + 1)
+            multiply(y_first, z_first[pair][:, row, :], g_first[pair][:, row, :], slice(r, r + 1), 0, HALF)
+        multiply(y_third, z_third[:], g_third[:], slice(0, PACK), THIRD, LAST)
+        multiply(y_last, z_last[:], g_last[:], slice(0, PACK), LAST, QUERIES)
 
         nc.gpsimd.tensor_scalar(
             y_bf[:, 0 : CHUNK * PACK].rearrange("p (q t) -> p q t", t=PACK),

@@ -47,9 +47,9 @@ def tile_attend_plh_swiglu_topk_kernel(tc, qT, k_words, k_scales, c_words, c_sca
 
         nc.vector.memset(ks[:].bitcast(I32), 0)
         nc.vector.memset(cs[0:COMPACT, :].bitcast(I32), 0)
-        nc.sync.dma_start(offsets[:], offs)
-        nc.scalar.dma_start(cs[COMPACT:P, :].bitcast(I32), c_scales[0].bitcast(I32))
         nc.sync.dma_start(q_first[:], q_rows[:, :, 0:HALF])
+        nc.scalar.dma_start(cs[COMPACT:P, :].bitcast(I32), c_scales[0].bitcast(I32))
+        nc.sync.dma_start(offsets[:], offs)
         for i in range(BLOCKS // QUADS):
             nc.sync.dma_start(ks[i:P:32, :].bitcast(I32), k_scales[0, i:BLOCKS:QUADS, :].bitcast(I32))
         nc.sync.dma_start(kw[:], k_words[0].rearrange("p n t -> p (n t)").bitcast(I32))

@@ -117,19 +117,24 @@ def tile_attend_plh_swiglu_topk_kernel(tc, qT, k_words, k_scales, c_words, c_sca
         round_to_words(nc.scalar.copy, q_bf_first, 0, q_first[:])
         quantise_q(q_bf_first, 0, HALF)
 
-        k_dealt = gather_dealt(kw, U32, "k_dealt")
-        a_first = {r: product(f"a_first{r}", k_dealt, k_plane, (r, r + 1), 0, HALF) for r in (0, 2)}
-        warm = psum.tile([P, LAST], F32, name="warm", tag="z_last")
-        for start, width in ((0, HALF), (HALF, CHUNK)):
+        warm = psum.tile([P, SLOTS], F32, name="warm", tag="z_last")
+
+        def warm_up(words, plane):
             nc.tensor.matmul_mx(
-                warm[:, start : start + width],
-                lhsT=k_dealt[:, 0:P].bitcast(FP8X4),
-                lhsT_scale=k_plane[:, 0:P],
-                rhs=q_codes[:, 0:width].bitcast(FP8X4),
-                rhs_scale=q_scale[:, 0:width],
+                warm[0:32, 0 : words.shape[1]],
+                lhsT=words[:, 0:32].bitcast(FP8X4),
+                lhsT_scale=plane[:, 0:32],
+                rhs=words.bitcast(FP8X4),
+                rhs_scale=plane,
                 start=True,
                 stop=True,
             )
+
+        for w in range(7):
+            warm_up(q_codes[:, 0:CHUNK], k_plane[:, 0:CHUNK])
+        k_dealt = gather_dealt(kw, U32, "k_dealt")
+        a_first = {r: product(f"a_first{r}", k_dealt, k_plane, (r, r + 1), 0, HALF) for r in (0, 2)}
+        warm_up(k_dealt[:], k_plane[:])
         g_first = {0: gate(a_first[0], "g_first0")}
         c_dealt = gather_dealt(cw, U32, "c_dealt")
 

from contextlib import ExitStack

import concourse.mybir as mybir

F32 = mybir.dt.float32
BF16 = mybir.dt.bfloat16
I32 = mybir.dt.int32
U32 = mybir.dt.uint32
U16 = mybir.dt.uint16
U8 = mybir.dt.uint8
FP8X4 = mybir.dt.float8_e4m3fn_x4
ACT = mybir.ActivationFunctionType
MULT = mybir.AluOpType.mult
ADD = mybir.AluOpType.add

P = 128
PACK = 4
QUADS = 4
SLOTS = 512
NEURONS = 2048
QUERIES = 512
BLOCKS = 16
COMPACT = P - BLOCKS
CHUNK = 128
HALF = 256
THIRD = HALF
LAST = HALF + CHUNK
LAST_Q_ON_VECTOR = 32
LAST_Y_ON_SCALAR = 64

FLOPS = 2 * 2 * 512 * 512 * 512


def tile_attend_plh_swiglu_topk_kernel(tc, qT, k_words, k_scales, c_words, c_scales, offs, out_0, out_1, out_2):
    nc = tc.nc
    with ExitStack() as ctx:
        keep = ctx.enter_context(tc.tile_pool(name="keep", bufs=1))
        psum = ctx.enter_context(tc.psum_pool(name="psum", bufs=1))

        offsets = keep.tile([P, SLOTS // 16], U16, name="offsets")
        kw = keep.tile([P, NEURONS], I32, name="kw", align_bytes=64)
        cw = keep.tile([P, NEURONS], I32, name="cw")
        ks = keep.tile([P, NEURONS], U8, name="ks", align_bytes=64)
        cs = keep.tile([P, NEURONS], U8, name="cs", tag="cs_then_q")
        q_first = keep.tile([P, PACK, HALF], F32, name="q_first")
        q_rows = qT[0].rearrange("(p t) q -> p t q", t=PACK)

        nc.vector.memset(ks[:].bitcast(I32), 0)
        nc.vector.memset(cs[0:COMPACT, :].bitcast(I32), 0)
        nc.sync.dma_start(q_first[:], q_rows[:, :, 0:HALF])
        nc.scalar.dma_start(cs[COMPACT:P, :].bitcast(I32), c_scales[0].bitcast(I32))
        nc.sync.dma_start(offsets[:], offs)
        for i in range(BLOCKS // QUADS):
            nc.sync.dma_start(ks[i:P:32, :].bitcast(I32), k_scales[0, i:BLOCKS:QUADS, :].bitcast(I32))
        nc.sync.dma_start(kw[:], k_words[0].rearrange("p n t -> p (n t)").bitcast(I32))
        nc.sync.dma_start(cw[:], c_words[0].rearrange("p n t -> p (n t)").bitcast(I32))

        def gather_dealt(table, dtype, name):
            dealt = keep.tile([P, SLOTS], dtype, name=name, align_bytes=64)
            nc.vector.tensor_copy(dealt[:].rearrange("p (r s) -> p s r", r=PACK), table[:].bitcast(dtype).indirect(offsets[:]))
            return dealt

        c_plane = keep.tile([P, SLOTS], U8, name="c_plane", align_bytes=64)
        nc.vector.memset(c_plane[:].bitcast(I32), 0)
        c_compact = gather_dealt(cs, U8, "c_compact")
        for quad in range(QUADS):
            src = COMPACT + 4 * quad
            nc.sync.dma_start(c_plane[32 * quad : 32 * quad + 4, :].bitcast(I32), c_compact[src : src + 4, :].bitcast(I32))
        q_late = keep.tile([P, PACK, HALF], F32, name="q_late", tag="cs_then_q")
        nc.sync.dma_start(q_late[:], q_rows[:, :, HALF:QUERIES])
        k_plane = gather_dealt(ks, U8, "k_plane")

        q_codes = keep.tile([P, QUERIES], U32, name="q_codes", align_bytes=64)
        q_scale = keep.tile([P, QUERIES], U8, name="q_scale", align_bytes=64)
        y_bf = keep.tile([P, QUERIES * PACK], BF16, name="y_bf", align_bytes=64)
        y_codes = keep.tile([P, QUERIES], U32, name="y_codes", align_bytes=64)
        y_scale = keep.tile([P, QUERIES], U8, name="y_scale", align_bytes=64)
        q_bf_third = keep.tile([P, CHUNK * PACK], BF16, name="q_bf_third", tag="q_then_y", align_bytes=64)
        q_bf_last = keep.tile([P, CHUNK * PACK], BF16, name="q_bf_last", align_bytes=64)
        q_bf_first = keep.tile([P, HALF * PACK], BF16, name="q_bf_first", align_bytes=64)
        out_rows = out_0.rearrange("(p r) q -> p r q", r=PACK)
        words_out = out_1[0].rearrange("p q u -> p (q u)").bitcast(I32)

        def round_to_words(copy, dst, lo, src):
            part = dst[:, lo * PACK : (lo + src.shape[2]) * PACK]
            copy(part.rearrange("p (c i t) -> p c t i", i=4, t=PACK), src.rearrange("p t (c i) -> p c t i", i=4))

        def quantise_q(q_bf, lo, hi):
            nc.vector.quantize_mx(q_codes[:, lo:hi].bitcast(FP8X4), q_scale[:, lo:hi], q_bf[:])

        def quantise_y(lo, hi):
            nc.vector.quantize_mx(y_codes[:, lo:hi].bitcast(FP8X4), y_scale[:, lo:hi], y_bf[:, lo * PACK : hi * PACK])

        def product(name, words, plane, rows, lo, hi):
            bank = psum.tile([P, len(rows), hi - lo], F32, name=name)
            for j, r in enumerate(rows):
                nc.tensor.matmul_mx(
                    bank[:, j, :],
                    lhsT=words[:, r * P : (r + 1) * P].bitcast(FP8X4),
                    lhsT_scale=plane[:, r * P : (r + 1) * P],
                    rhs=q_codes[:, lo:hi].bitcast(FP8X4),
                    rhs_scale=q_scale[:, lo:hi],
                    start=True,
                    stop=True,
                )
            return bank

        def gate(bank, name, tag=""):
            gates = keep.tile(list(bank.shape), F32, name=name, tag=tag)
            nc.scalar.activation(gates[:], bank[:], ACT.Silu)
            return gates

        def multiply(y, bank, gates, rows, lo, hi):
            nc.vector.tensor_tensor(y[:, rows, :], bank, gates, MULT)
            nc.sync.dma_start(out_rows[:, rows, lo:hi], y[:, rows, :])

        round_to_words(nc.scalar.copy, q_bf_first, 0, q_first[:])
        quantise_q(q_bf_first, 0, HALF)

        warm = psum.tile([P, SLOTS], F32, name="warm", tag="z_last")

        def warm_up(words, plane):
            nc.tensor.matmul_mx(
                warm[0:32, 0 : words.shape[1]],
                lhsT=words[:, 0:32].bitcast(FP8X4),
                lhsT_scale=plane[:, 0:32],
                rhs=words.bitcast(FP8X4),
                rhs_scale=plane,
                start=True,
                stop=True,
            )

        for w in range(7):
            warm_up(q_codes[:, 0:CHUNK], k_plane[:, 0:CHUNK])
        k_dealt = gather_dealt(kw, U32, "k_dealt")
        a_first = {r: product(f"a_first{r}", k_dealt, k_plane, (r, r + 1), 0, HALF) for r in (0, 2)}
        warm_up(k_dealt[:], k_plane[:])
        g_first = {0: gate(a_first[0], "g_first0")}
        c_dealt = gather_dealt(cw, U32, "c_dealt")

        round_to_words(nc.vector.tensor_copy, q_bf_third, 0, q_late[:, :, 0:CHUNK])
        round_to_words(nc.vector.tensor_copy, q_bf_last, 0, q_late[:, :, CHUNK : CHUNK + LAST_Q_ON_VECTOR])
        round_to_words(nc.scalar.copy, q_bf_last, LAST_Q_ON_VECTOR, q_late[:, :, CHUNK + LAST_Q_ON_VECTOR : HALF])
        g_first[2] = gate(a_first[2], "g_first2", tag="cs_then_q")
        quantise_q(q_bf_third, THIRD, LAST)
        quantise_q(q_bf_last, LAST, QUERIES)

        z_first = {0: product("z_first0", c_dealt, c_plane, (0, 1), 0, HALF)}
        a_third = product("a_third", k_dealt, k_plane, range(PACK), THIRD, LAST)
        z_first[2] = product("z_first2", c_dealt, c_plane, (2, 3), 0, HALF)
        a_last = product("a_last", k_dealt, k_plane, range(PACK), LAST, QUERIES)
        g_third = gate(a_third, "g_third")
        g_last = gate(a_last, "g_last")
        z_third = product("z_third", c_dealt, c_plane, range(PACK), THIRD, LAST)
        z_last = product("z_last", c_dealt, c_plane, range(PACK), LAST, QUERIES)

        y_first = keep.tile([P, PACK, HALF], F32, name="y_first", tag="q_then_y", align_bytes=64)
        y_third = keep.tile([P, PACK, CHUNK], F32, name="y_third")
        y_last = keep.tile([P, PACK, CHUNK], F32, name="y_last")
        for r in range(PACK):
            pair, row = r - r % 2, slice(r % 2, r % 2 + 1)
            multiply(y_first, z_first[pair][:, row, :], g_first[pair][:, row, :], slice(r, r + 1), 0, HALF)
        multiply(y_third, z_third[:], g_third[:], slice(0, PACK), THIRD, LAST)
        multiply(y_last, z_last[:], g_last[:], slice(0, PACK), LAST, QUERIES)

        nc.gpsimd.tensor_scalar(
            y_bf[:, 0 : CHUNK * PACK].rearrange("p (q t) -> p q t", t=PACK),
            y_first[:, :, 0:CHUNK].rearrange("p t q -> p q t"),
            1.0,
            -0.0,
            MULT,
            ADD,
        )
        round_to_words(nc.scalar.copy, y_bf, CHUNK, y_first[:, :, CHUNK:HALF])
        round_to_words(nc.scalar.copy, y_bf, THIRD, y_third[:])
        quantise_y(0, HALF)
        round_to_words(nc.scalar.copy, y_bf, LAST, y_last[:, :, 0:LAST_Y_ON_SCALAR])
        round_to_words(nc.vector.tensor_copy, y_bf, LAST + LAST_Y_ON_SCALAR, y_last[:, :, LAST_Y_ON_SCALAR:CHUNK])
        quantise_y(THIRD, LAST)
        quantise_y(LAST, QUERIES)
        nc.sync.dma_start(words_out, y_codes[:].bitcast(I32))
        for quad in range(QUADS):
            queue = nc.scalar if quad % 2 == 0 else nc.sync
            queue.dma_start(out_2[0, 4 * quad : 4 * quad + 4, :].bitcast(I32), y_scale[32 * quad : 32 * quad + 4, :].bitcast(I32))
